import numpy as np
import ml_dtypes


def mxq(x, axis, fmt="e4m3"):
    dtype, down = {"e4m3": (ml_dtypes.float8_e4m3fn, 7), "e5m2": (ml_dtypes.float8_e5m2, 14)}[fmt]
    v = np.moveaxis(np.asarray(x, np.float32).astype(ml_dtypes.bfloat16).astype(np.float64), axis, -1)
    blocks = v.reshape(v.shape[:-1] + (-1, 32))
    amax = np.abs(blocks).max(-1, keepdims=True)
    byte = np.maximum(np.where(amax > 0, np.frexp(amax)[1] - 1 + 127, 0) - down, 1)
    scale = np.exp2(byte - 127.0)
    codes = (blocks / scale).astype(np.float32).astype(dtype).astype(np.float64)
    return np.moveaxis((codes * scale).reshape(v.shape), -1, axis)


WIDE = False


def mx_kscale(k):
    if not WIDE:
        return np.ones(k)
    levels = np.array([10, -10, 5, -5, 0])
    if k % 512:
        return np.exp2(np.random.permutation(np.resize(levels, k // 32))).repeat(32)
    a = np.empty((k // 512, 16))
    for p in range(k // 512):
        a[p, :8] = np.random.permutation(np.resize(levels, 8))
        for g in range(8):
            far = levels[np.abs(levels - a[p, g]) >= 10]
            a[p, g + 8] = far[np.random.randint(len(far))]
    return np.exp2(a.ravel()).repeat(32)


def f64(x):
    return np.asarray(x).astype(np.float64)


def striped(idx):
    return np.tile(idx.reshape(-1, 16).T, (8, 1)).astype(np.uint16)


def unstriped(offs):
    return offs[:16].T.reshape(-1).astype(np.int64)


def pack_weight(w):
    k, n = w.shape
    w = f64(np.asarray(w, np.float32).astype(ml_dtypes.bfloat16)).reshape(k // 32, 32, n)
    amax = np.abs(w).max(1)
    byte = np.clip(np.where(amax > 0, np.frexp(amax)[1] - 1 + 127 - 7, 1), 1, 254)
    scaled = (w * np.exp2(127.0 - byte)[:, None, :]).reshape(k, n).astype(np.float32)
    words = np.ascontiguousarray(scaled.reshape(k // 512, 128, 4, n).transpose(0, 1, 3, 2)).astype(ml_dtypes.float8_e4m3fn).view(np.uint8)
    return words, np.ascontiguousarray(byte.astype(np.uint8).reshape(k // 512, 16, n))


def unpack_weight(words, scales):
    g, p, n, _ = words.shape
    vals = np.ascontiguousarray(words).view(ml_dtypes.float8_e4m3fn).astype(np.float64) * np.repeat(np.exp2(scales.astype(np.float64) - 127.0), 8, axis=1)[..., None]
    return vals.transpose(0, 1, 3, 2).reshape(g * 512, n)


def silu(v):
    return v / (1.0 + np.exp(-np.maximum(v, -700.0)))


K, T, S, H, N, U = 1024, 2048, 1024, 512, 256, 1024


def setup_inputs():
    n = np.random.standard_normal
    s = mx_kscale(K)[:, None]
    u = mx_kscale(H)
    packed_xT = pack_weight(n((K, T)) * s)
    packed_w3 = pack_weight(n((H, N)) / np.sqrt(H) / u[:, None])
    return {
        "x_words": packed_xT[0],
        "x_scales": packed_xT[1],
        "w1": (n((K, H)) / np.sqrt(2 * K) / s * u).astype(np.float32),
        "w2": (n((K, H)) / np.sqrt(2 * K) / s * u).astype(np.float32),
        "w3_words": packed_w3[0],
        "w3_scales": packed_w3[1],
        "offs": striped(np.random.permutation(T)[:S]),
        "src": striped(np.random.permutation(S)[(S * np.random.uniform(0, 1, U) ** 4).astype(np.int64)]),
        "dst": striped(np.random.permutation(S)),
    }


def reference(x_words, x_scales, w1, w2, w3_words, w3_scales, offs, src, dst):
    xq = unpack_weight(x_words, x_scales)[:, unstriped(offs)]
    y = mxq(f64(w1), 0, "e4m3").T @ xq
    e = mxq(f64(w2), 0, "e4m3").T @ xq
    z = silu(y[:, unstriped(src)] + e[:, unstriped(dst)])
    return unpack_weight(w3_words, w3_scales).T @ mxq(z, 0, "e4m3")

@@ -1,0 +1,244 @@
+from contextlib import ExitStack
+
+import concourse.mybir as mybir
+
+K, T, S, H, N, U = 1024, 2048, 1024, 512, 256, 1024
+FLOPS = 2 * (2 * K * H * S + H * N * U)
+
+F32 = mybir.dt.float32
+BF16 = mybir.dt.bfloat16
+I32 = mybir.dt.int32
+U32 = mybir.dt.uint32
+U16 = mybir.dt.uint16
+U8 = mybir.dt.uint8
+FP8X4 = mybir.dt.float8_e4m3fn_x4
+ADD = mybir.AluOpType.add
+SILU = mybir.ActivationFunctionType.Silu
+
+P = 128
+PACK = 4
+K_PASS = P * PACK
+PASSES = K // K_PASS
+BANK = 512
+HALVES = S // BANK
+LIST_ROWS = 16
+QUADRANT = 32
+SCALE_ROWS = 4
+EDGE_SLICES = ((0, 512), (512, 768), (768, 896), (896, 1024))
+
+
+def entries(list_tile, first, last):
+    return list_tile[:, first // LIST_ROWS : last // LIST_ROWS]
+
+
+def tile_picked_hub_silu_p_kernel(
+    tc, x_words, x_scales, w1, w2, w3_words, w3_scales, offs, src, dst, out
+):
+    nc = tc.nc
+    with ExitStack() as ctx:
+        lists = ctx.enter_context(tc.tile_pool(name="lists", bufs=1))
+        keep = ctx.enter_context(tc.tile_pool(name="keep", bufs=1))
+        psum = ctx.enter_context(tc.psum_pool(name="psum", bufs=8))
+
+        offs_t = lists.tile([P, S // LIST_ROWS], U16, name="offs_t")
+        src_t = lists.tile([P, U // LIST_ROWS], U16, name="src_t")
+        dst_t = lists.tile([P, U // LIST_ROWS], U16, name="dst_t")
+
+        xs_all = keep.tile([P, T], U8, name="xs_all", align_bytes=64)
+        w3_s = keep.tile([P, N], U8, name="w3_s", align_bytes=64)
+        w3_c = keep.tile([P, N], U32, name="w3_c", align_bytes=64)
+        warm = keep.tile([P, 2], F32, name="warm")
+        nc.vector.memset(xs_all[:].bitcast(I32), 0)
+        nc.vector.memset(w3_s[:].bitcast(I32), 0)
+
+        xw_all = [keep.tile([P, T], U32, name=f"xw_all{g}", align_bytes=64) for g in range(PASSES)]
+        raw = {
+            (a, g): keep.tile([P, PACK, H], F32, name=f"raw{a}{g}", align_bytes=64)
+            for a in range(2)
+            for g in range(PASSES)
+        }
+
+        def load_words(g):
+            nc.sync.dma_start(
+                out=xw_all[g][:].bitcast(I32), in_=x_words[g].rearrange("p n t -> p (n t)").bitcast(I32)
+            )
+
+        def load_weight(a, g):
+            rows = (w1, w2)[a][g * K_PASS : (g + 1) * K_PASS, :]
+            nc.sync.dma_start(out=raw[a, g][:], in_=rows.rearrange("(p j) c -> p j c", j=PACK))
+
+        nc.sync.dma_start(offs_t[:], offs)
+        for q in range(P // QUADRANT):
+            nc.sync.dma_start(
+                out=xs_all[QUADRANT * q : QUADRANT * q + PASSES * SCALE_ROWS, :].bitcast(I32),
+                in_=x_scales[:, SCALE_ROWS * q : SCALE_ROWS * (q + 1), :].bitcast(I32),
+            )
+        load_words(0)
+        load_weight(0, 0)
+        load_words(1)
+        load_weight(0, 1)
+        nc.sync.dma_start(src_t[:], src)
+        load_weight(1, 0)
+        load_weight(1, 1)
+        nc.sync.dma_start(dst_t[:], dst)
+        nc.sync.dma_start(out=w3_c[:].bitcast(I32), in_=w3_words[0].rearrange("p n t -> p (n t)").bitcast(I32))
+        for q in range(P // QUADRANT):
+            nc.sync.dma_start(
+                out=w3_s[QUADRANT * q : QUADRANT * q + SCALE_ROWS, :].bitcast(I32),
+                in_=w3_scales[0, SCALE_ROWS * q : SCALE_ROWS * (q + 1), :].bitcast(I32),
+            )
+
+        nc.gpsimd.memset(warm[:, 0:1], 0.0)
+        nc.scalar.activation(out=warm[:, 1:2], in_=warm[:, 0:1], func=SILU)
+
+        xs = keep.tile([P, S], U8, name="xs", align_bytes=64)
+        xw = {}
+        codes, scales = {}, {}
+
+        def gather_words(g, tag):
+            xw[g] = keep.tile([P, S], U32, name=f"xw{g}", tag=tag, align_bytes=64)
+            nc.vector.tensor_copy(out=xw[g][:], in_=xw_all[g][:].indirect(offs_t[:]))
+
+        def weave(a, g, pair, engine, tag):
+            woven = keep.tile([P, 2, P, PACK], BF16, name=f"woven{a}{g}{pair}", tag=tag, align_bytes=64)
+            o = woven[:].rearrange("p t m j -> p m j t")
+            i = raw[a, g][:].rearrange("p j (m t) -> p m j t", t=PACK)[:, :, :, 2 * pair : 2 * pair + 2]
+            if engine == "scalar":
+                nc.scalar.copy(out=o, in_=i)
+            else:
+                nc.vector.tensor_copy(out=o, in_=i)
+            return woven
+
+        def quantise(a, g, pair, woven):
+            c = keep.tile([P, 2 * P], U32, name=f"codes{a}{g}{pair}", align_bytes=64)
+            s = keep.tile([P, 2 * P], U8, name=f"scales{a}{g}{pair}", align_bytes=64)
+            nc.vector.quantize_mx(out=c[:].bitcast(FP8X4), scales=s[:], in_=woven[:].rearrange("p t m j -> p (t m j)"))
+            codes[a, g, pair], scales[a, g, pair] = c, s
+
+        banks = {}
+
+        def product_pass(a, g, t, h):
+            if g == 0:
+                banks[a, t, h] = psum.tile([P, BANK], F32, name=f"bank{a}{t}{h}", tag="bank")
+            cols = slice((t % 2) * P, (t % 2 + 1) * P)
+            picked = slice(h * BANK, (h + 1) * BANK)
+            nc.tensor.matmul_mx(
+                out=banks[a, t, h][:],
+                lhsT=codes[a, g, t // 2][:, cols].bitcast(FP8X4),
+                lhsT_scale=scales[a, g, t // 2][:, cols],
+                rhs=xw[g][:, picked].bitcast(FP8X4),
+                rhs_scale=xs[SCALE_ROWS * g :, picked],
+                start=(g == 0),
+                stop=(g == PASSES - 1),
+            )
+
+        rows = {(a, t): keep.tile([P, S], F32, name=f"rows{a}{t}", align_bytes=64) for a in range(2) for t in range(PACK)}
+
+        def empty_bank(a, t, h, engine="scalar"):
+            o = rows[a, t][:, h * BANK : (h + 1) * BANK]
+            if engine == "scalar":
+                nc.scalar.copy(out=o, in_=banks[a, t, h][:])
+            else:
+                nc.vector.tensor_copy(out=o, in_=banks[a, t, h][:])
+
+        fetched = {}
+
+        def fetch_sources(t, tags):
+            for h in range(2):
+                first, last = h * U // 2, (h + 1) * U // 2
+                fetched[t, h] = keep.tile([P, U // 2], F32, name=f"fetched{t}{h}", tag=tags[h], align_bytes=64)
+                nc.vector.tensor_copy(out=fetched[t, h][:], in_=rows[0, t][:].indirect(entries(src_t, first, last)))
+
+        nc.vector.tensor_copy(out=xs[:], in_=xs_all[:].indirect(offs_t[:]))
+        gather_words(0, "xw0")
+        wa = weave(0, 0, 0, "scalar", "wa")
+        wb = weave(0, 0, 1, "scalar", "wb")
+        quantise(0, 0, 0, wa)
+        gather_words(1, "wa")
+        wb0 = wb
+        for t in range(2):
+            for h in range(HALVES):
+                product_pass(0, 0, t, h)
+        wa = weave(0, 1, 0, "vector", "wc")
+        wb = weave(0, 1, 1, "scalar", "wd")
+        quantise(0, 0, 1, wb0)
+        quantise(0, 1, 0, wa)
+        quantise(0, 1, 1, wb)
+        for t in range(2):
+            for h in range(HALVES):
+                product_pass(0, 1, t, h)
+        for t in range(2, PACK):
+            for h in range(HALVES):
+                for g in range(PASSES):
+                    product_pass(0, g, t, h)
+        empty_bank(0, 0, 0)
+        empty_bank(0, 0, 1, "vector")
+        fetch_sources(0, ("f00", "f01"))
+        empty_bank(0, 1, 0)
+        empty_bank(0, 1, 1)
+        fetch_sources(1, ("f10", "f11"))
+        wa = weave(1, 0, 0, "scalar", "we")
+        wb = weave(1, 0, 1, "scalar", "wf")
+        empty_bank(0, 2, 0)
+        empty_bank(0, 2, 1)
+        quantise(1, 0, 0, wa)
+        quantise(1, 0, 1, wb)
+        fetch_sources(2, ("wf", "we"))
+        wa = weave(1, 1, 0, "scalar", "wg")
+        wb = weave(1, 1, 1, "scalar", "wh")
+        empty_bank(0, 3, 0)
+        empty_bank(0, 3, 1)
+        quantise(1, 1, 0, wa)
+        quantise(1, 1, 1, wb)
+        fetch_sources(3, ("wh", "wg"))
+        for t in range(PACK):
+            for h in range(HALVES):
+                for g in range(PASSES):
+                    product_pass(1, g, t, h)
+                empty_bank(1, t, h)
+
+        out_v = out.rearrange("(mt p) r -> p mt r", p=P)
+
+        sums = {}
+
+        def join(first, last):
+            n = last - first
+            h, at = divmod(first, U // 2)
+            if at == 0:
+                sums[h] = keep.tile([P, PACK * U // 2], F32, name=f"sums{h}", tag=("u0", "wh")[h], align_bytes=64)
+            u = sums[h][:, PACK * at : PACK * (at + n)].rearrange("p (t r) -> p t r", t=PACK)
+            for t in range(PACK):
+                nc.vector.tensor_tensor(
+                    out=u[:, t, :], in0=rows[1, t][:].indirect(entries(dst_t, first, last)), in1=fetched[t, h][:, at : at + n], op=ADD
+                )
+            z = keep.tile([P, n, PACK], BF16, name=f"z{first}", align_bytes=64)
+            nc.scalar.activation(
+                out=z[:].rearrange("p (c i) t -> p c t i", i=4), in_=u.rearrange("p t (c i) -> p c t i", i=4), func=SILU
+            )
+            return z
+
+        def finish(first, last, z):
+            n = last - first
+            zc = keep.tile([P, n], U32, name=f"zc{first}", align_bytes=64)
+            zs = keep.tile([P, n], U8, name=f"zs{first}", align_bytes=64)
+            nc.vector.quantize_mx(out=zc[:].bitcast(FP8X4), scales=zs[:], in_=z[:].rearrange("p r t -> p (r t)"))
+            res = keep.tile([P, N // P, n], F32, name=f"res{first}", align_bytes=64)
+            per_bank = min(N // P, BANK // n)
+            for b in range(N // P // per_bank):
+                acc = psum.tile([P, per_bank, n], F32, name=f"acc{first}{b}", tag="bank")
+                for i in range(per_bank):
+                    cols = slice((b * per_bank + i) * P, (b * per_bank + i + 1) * P)
+                    nc.tensor.matmul_mx(
+                        out=acc[:, i, :], lhsT=w3_c[:, cols].bitcast(FP8X4), lhsT_scale=w3_s[:, cols],
+                        rhs=zc[:].bitcast(FP8X4), rhs_scale=zs[:], start=True, stop=True,
+                    )
+                nc.scalar.copy(out=res[:, b * per_bank : (b + 1) * per_bank, :], in_=acc[:])
+            nc.sync.dma_start(out=out_v[:, :, first:last], in_=res[:])
+
+        waiting = None
+        for first, last in EDGE_SLICES:
+            z = join(first, last)
+            if waiting is not None:
+                finish(*waiting)
+            waiting = (first, last, z)
+        finish(*waiting)

@@ -24,7 +24,9 @@ HALVES = S // BANK
 LIST_ROWS = 16
 QUADRANT = 32
 SCALE_ROWS = 4
-EDGE_SLICES = ((0, 512), (512, 768), (768, 896), (896, 1024))
+EDGE_SLICE = 256
+Y_WINDOW = 1376
+E_WINDOW = S + LIST_ROWS
 
 
 def entries(list_tile, first, last):
@@ -132,7 +134,13 @@ def tile_picked_hub_silu_p_kernel(
                 stop=(g == PASSES - 1),
             )
 
-        rows = {(a, t): keep.tile([P, S], F32, name=f"rows{a}{t}", align_bytes=64) for a in range(2) for t in range(PACK)}
+        y_all = keep.tile([P, (PACK - 1) * S + Y_WINDOW], F32, name="y_all", align_bytes=64)
+        nc.gpsimd.memset(y_all[:, PACK * S :], 0.0)
+        e_all = [keep.tile([P, E_WINDOW if t < PACK - 1 else S], F32, name=f"e_all{t}", align_bytes=64) for t in range(PACK)]
+        for t in range(PACK - 1):
+            nc.gpsimd.memset(e_all[t][:, S:], 0.0)
+        rows = {(0, t): y_all[:, (PACK - 1 - t) * S : (PACK - t) * S] for t in range(PACK)}
+        rows.update({(1, t): e_all[t][:, :S] for t in range(PACK)})
 
         def empty_bank(a, t, h, engine="scalar"):
             o = rows[a, t][:, h * BANK : (h + 1) * BANK]
@@ -143,11 +151,10 @@ def tile_picked_hub_silu_p_kernel(
 
         fetched = {}
 
-        def fetch_sources(t, tags):
-            for h in range(2):
-                first, last = h * U // 2, (h + 1) * U // 2
-                fetched[t, h] = keep.tile([P, U // 2], F32, name=f"fetched{t}{h}", tag=tags[h], align_bytes=64)
-                nc.vector.tensor_copy(out=fetched[t, h][:], in_=rows[0, t][:].indirect(entries(src_t, first, last)))
+        def fetch_sources(t, tag):
+            fetched[t] = keep.tile([P, U], F32, name=f"fetched{t}", tag=tag, align_bytes=64)
+            at = (PACK - 1 - t) * S
+            nc.vector.tensor_copy(out=fetched[t][:], in_=y_all[:, at : at + Y_WINDOW].indirect(src_t[:]))
 
         nc.vector.tensor_copy(out=xs[:], in_=xs_all[:].indirect(offs_t[:]))
         gather_words(0, "xw0")
@@ -173,24 +180,24 @@ def tile_picked_hub_silu_p_kernel(
                     product_pass(0, g, t, h)
         empty_bank(0, 0, 0)
         empty_bank(0, 0, 1, "vector")
-        fetch_sources(0, ("f00", "f01"))
+        fetch_sources(0, "f0")
         empty_bank(0, 1, 0)
         empty_bank(0, 1, 1)
-        fetch_sources(1, ("f10", "f11"))
+        fetch_sources(1, "f1")
         wa = weave(1, 0, 0, "scalar", "we")
         wb = weave(1, 0, 1, "scalar", "wf")
         empty_bank(0, 2, 0)
         empty_bank(0, 2, 1)
         quantise(1, 0, 0, wa)
         quantise(1, 0, 1, wb)
-        fetch_sources(2, ("wf", "we"))
+        fetch_sources(2, "wf")
         wa = weave(1, 1, 0, "scalar", "wg")
         wb = weave(1, 1, 1, "scalar", "wh")
         empty_bank(0, 3, 0)
         empty_bank(0, 3, 1)
         quantise(1, 1, 0, wa)
         quantise(1, 1, 1, wb)
-        fetch_sources(3, ("wh", "wg"))
+        fetch_sources(3, "wh")
         for t in range(PACK):
             for h in range(HALVES):
                 for g in range(PASSES):
@@ -199,46 +206,59 @@ def tile_picked_hub_silu_p_kernel(
 
         out_v = out.rearrange("(mt p) r -> p mt r", p=P)
 
-        sums = {}
+        u = keep.tile([P, PACK, U], F32, name="u", align_bytes=64)
+        z = keep.tile([P, U, PACK], BF16, name="z", align_bytes=64)
 
-        def join(first, last):
-            n = last - first
-            h, at = divmod(first, U // 2)
-            if at == 0:
-                sums[h] = keep.tile([P, PACK * U // 2], F32, name=f"sums{h}", tag=("u0", "wh")[h], align_bytes=64)
-            u = sums[h][:, PACK * at : PACK * (at + n)].rearrange("p (t r) -> p t r", t=PACK)
-            for t in range(PACK):
-                nc.vector.tensor_tensor(
-                    out=u[:, t, :], in0=rows[1, t][:].indirect(entries(dst_t, first, last)), in1=fetched[t, h][:, at : at + n], op=ADD
-                )
-            z = keep.tile([P, n, PACK], BF16, name=f"z{first}", align_bytes=64)
-            nc.scalar.activation(
-                out=z[:].rearrange("p (c i) t -> p c t i", i=4), in_=u.rearrange("p t (c i) -> p c t i", i=4), func=SILU
+        def join(t, first, last):
+            nc.vector.tensor_tensor(
+                out=u[:, t, first:last], in0=e_all[t][:].indirect(entries(dst_t, first, last)), in1=fetched[t][:, first:last], op=ADD
             )
-            return z
 
-        def finish(first, last, z):
-            n = last - first
-            zc = keep.tile([P, n], U32, name=f"zc{first}", align_bytes=64)
-            zs = keep.tile([P, n], U8, name=f"zs{first}", align_bytes=64)
-            nc.vector.quantize_mx(out=zc[:].bitcast(FP8X4), scales=zs[:], in_=z[:].rearrange("p r t -> p (r t)"))
-            res = keep.tile([P, N // P, n], F32, name=f"res{first}", align_bytes=64)
-            per_bank = min(N // P, BANK // n)
-            for b in range(N // P // per_bank):
-                acc = psum.tile([P, per_bank, n], F32, name=f"acc{first}{b}", tag="bank")
-                for i in range(per_bank):
-                    cols = slice((b * per_bank + i) * P, (b * per_bank + i + 1) * P)
-                    nc.tensor.matmul_mx(
-                        out=acc[:, i, :], lhsT=w3_c[:, cols].bitcast(FP8X4), lhsT_scale=w3_s[:, cols],
-                        rhs=zc[:].bitcast(FP8X4), rhs_scale=zs[:], start=True, stop=True,
-                    )
-                nc.scalar.copy(out=res[:, b * per_bank : (b + 1) * per_bank, :], in_=acc[:])
-            nc.sync.dma_start(out=out_v[:, :, first:last], in_=res[:])
+        def activate(pair, first, last):
+            nc.scalar.activation(
+                out=z[:, first:last, 2 * pair : 2 * pair + 2],
+                in_=u[:, 2 * pair : 2 * pair + 2, first:last].rearrange("p t r -> p r t"),
+                func=SILU,
+            )
 
-        waiting = None
-        for first, last in EDGE_SLICES:
-            z = join(first, last)
-            if waiting is not None:
-                finish(*waiting)
-            waiting = (first, last, z)
-        finish(*waiting)
+        join(0, 0, U)
+        join(1, 0, U)
+        activate(0, 0, U)
+        join(2, 0, U)
+        starts = range(0, U, EDGE_SLICE)
+        for first in starts:
+            join(3, first, first + EDGE_SLICE)
+            activate(1, first, first + EDGE_SLICE)
+        zc, zs = {}, {}
+        for first in starts:
+            zc[first] = keep.tile([P, EDGE_SLICE], U32, name=f"zc{first}", align_bytes=64)
+            zs[first] = keep.tile([P, EDGE_SLICE], U8, name=f"zs{first}", align_bytes=64)
+            part = z[:, first : first + EDGE_SLICE, :].rearrange("p r t -> p (r t)")
+            nc.vector.quantize_mx(out=zc[first][:].bitcast(FP8X4), scales=zs[first][:], in_=part)
+
+        def last_product(acc, m, first):
+            cols = slice(m * P, (m + 1) * P)
+            nc.tensor.matmul_mx(
+                out=acc, lhsT=w3_c[:, cols].bitcast(FP8X4), lhsT_scale=w3_s[:, cols],
+                rhs=zc[first][:].bitcast(FP8X4), rhs_scale=zs[first][:], start=True, stop=True,
+            )
+
+        for i, first in enumerate(starts):
+            res = keep.tile([P, N // P, EDGE_SLICE], F32, name=f"res{first}", align_bytes=64)
+            if i < len(starts) - 1:
+                acc = psum.tile([P, N // P, EDGE_SLICE], F32, name=f"acc{first}", tag="bank")
+                for m in range(N // P):
+                    last_product(acc[:, m, :], m, first)
+                if i < 2:
+                    nc.scalar.copy(out=res[:], in_=acc[:])
+                else:
+                    nc.vector.tensor_copy(out=res[:], in_=acc[:])
+            else:
+                for m in range(N // P):
+                    acc = psum.tile([P, EDGE_SLICE], F32, name=f"acc{first}{m}", tag="bank")
+                    last_product(acc[:], m, first)
+                    if m == 0:
+                        nc.scalar.copy(out=res[:, m, :], in_=acc[:])
+                    else:
+                        nc.vector.tensor_copy(out=res[:, m, :], in_=acc[:])
+            nc.sync.dma_start(out=out_v[:, :, first : first + EDGE_SLICE], in_=res[:])

@@ -101,33 +101,35 @@ def tile_picked_hub_silu_p_kernel(
             xw[g] = keep.tile([P, S], U32, name=f"xw{g}", tag=tag, align_bytes=64)
             nc.vector.tensor_copy(out=xw[g][:], in_=xw_all[g][:].indirect(offs_t[:]))
 
-        def weave(a, g, pair, engine, tag):
-            woven = keep.tile([P, 2, P, PACK], BF16, name=f"woven{a}{g}{pair}", tag=tag, align_bytes=64)
+        def weave(a, g, first, count, engine, tag):
+            woven = keep.tile([P, count, P, PACK], BF16, name=f"woven{a}{g}{first}", tag=tag, align_bytes=64)
             o = woven[:].rearrange("p t m j -> p m j t")
-            i = raw[a, g][:].rearrange("p j (m t) -> p m j t", t=PACK)[:, :, :, 2 * pair : 2 * pair + 2]
+            i = raw[a, g][:].rearrange("p j (m t) -> p m j t", t=PACK)[:, :, :, first : first + count]
             if engine == "scalar":
                 nc.scalar.copy(out=o, in_=i)
             else:
                 nc.vector.tensor_copy(out=o, in_=i)
             return woven
 
-        def quantise(a, g, pair, woven):
-            c = keep.tile([P, 2 * P], U32, name=f"codes{a}{g}{pair}", align_bytes=64)
-            s = keep.tile([P, 2 * P], U8, name=f"scales{a}{g}{pair}", align_bytes=64)
+        def quantise(a, g, first, woven):
+            count = woven.shape[1]
+            c = keep.tile([P, count * P], U32, name=f"codes{a}{g}{first}", align_bytes=64)
+            s = keep.tile([P, count * P], U8, name=f"scales{a}{g}{first}", align_bytes=64)
             nc.vector.quantize_mx(out=c[:].bitcast(FP8X4), scales=s[:], in_=woven[:].rearrange("p t m j -> p (t m j)"))
-            codes[a, g, pair], scales[a, g, pair] = c, s
+            for i in range(count):
+                codes[a, g, first + i] = c[:, i * P : (i + 1) * P]
+                scales[a, g, first + i] = s[:, i * P : (i + 1) * P]
 
         banks = {}
 
         def product_pass(a, g, t, h):
             if g == 0:
                 banks[a, t, h] = psum.tile([P, BANK], F32, name=f"bank{a}{t}{h}", tag="bank")
-            cols = slice((t % 2) * P, (t % 2 + 1) * P)
             picked = slice(h * BANK, (h + 1) * BANK)
             nc.tensor.matmul_mx(
                 out=banks[a, t, h][:],
-                lhsT=codes[a, g, t // 2][:, cols].bitcast(FP8X4),
-                lhsT_scale=scales[a, g, t // 2][:, cols],
+                lhsT=codes[a, g, t].bitcast(FP8X4),
+                lhsT_scale=scales[a, g, t],
                 rhs=xw[g][:, picked].bitcast(FP8X4),
                 rhs_scale=xs[SCALE_ROWS * g :, picked],
                 start=(g == 0),
@@ -158,19 +160,19 @@ def tile_picked_hub_silu_p_kernel(
 
         nc.vector.tensor_copy(out=xs[:], in_=xs_all[:].indirect(offs_t[:]))
         gather_words(0, "xw0")
-        wa = weave(0, 0, 0, "scalar", "wa")
-        wb = weave(0, 0, 1, "scalar", "wb")
+        wa = weave(0, 0, 0, 2, "scalar", "wa")
+        wb = weave(0, 0, 2, 2, "scalar", "wb")
         quantise(0, 0, 0, wa)
         gather_words(1, "wa")
         wb0 = wb
         for t in range(2):
             for h in range(HALVES):
                 product_pass(0, 0, t, h)
-        wa = weave(0, 1, 0, "vector", "wc")
-        wb = weave(0, 1, 1, "scalar", "wd")
-        quantise(0, 0, 1, wb0)
+        wa = weave(0, 1, 0, 2, "vector", "wc")
+        wb = weave(0, 1, 2, 2, "scalar", "wd")
+        quantise(0, 0, 2, wb0)
         quantise(0, 1, 0, wa)
-        quantise(0, 1, 1, wb)
+        quantise(0, 1, 2, wb)
         for t in range(2):
             for h in range(HALVES):
                 product_pass(0, 1, t, h)
@@ -184,19 +186,15 @@ def tile_picked_hub_silu_p_kernel(
         empty_bank(0, 1, 0)
         empty_bank(0, 1, 1)
         fetch_sources(1, "f1")
-        wa = weave(1, 0, 0, "scalar", "we")
-        wb = weave(1, 0, 1, "scalar", "wf")
+        wa = weave(1, 0, 0, PACK, "scalar", "wf")
         empty_bank(0, 2, 0)
         empty_bank(0, 2, 1)
         quantise(1, 0, 0, wa)
-        quantise(1, 0, 1, wb)
         fetch_sources(2, "wf")
-        wa = weave(1, 1, 0, "scalar", "wg")
-        wb = weave(1, 1, 1, "scalar", "wh")
+        wa = weave(1, 1, 0, PACK, "scalar", "wh")
         empty_bank(0, 3, 0)
         empty_bank(0, 3, 1)
         quantise(1, 1, 0, wa)
-        quantise(1, 1, 1, wb)
         fetch_sources(3, "wh")
         for t in range(PACK):
             for h in range(HALVES):

@@ -24,7 +24,7 @@ HALVES = S // BANK
 LIST_ROWS = 16
 QUADRANT = 32
 SCALE_ROWS = 4
-EDGE_SLICE = 256
+EDGE_SLICES = ((0, 256), (256, 512), (512, 768), (768, 896), (896, 1024))
 Y_WINDOW = 1376
 E_WINDOW = S + LIST_ROWS
 
@@ -111,9 +111,9 @@ def tile_picked_hub_silu_p_kernel(
                 nc.vector.tensor_copy(out=o, in_=i)
             return woven
 
-        def quantise(a, g, first, woven):
+        def quantise(a, g, first, woven, tag=None):
             count = woven.shape[1]
-            c = keep.tile([P, count * P], U32, name=f"codes{a}{g}{first}", align_bytes=64)
+            c = keep.tile([P, count * P], U32, name=f"codes{a}{g}{first}", tag=tag or f"codes{a}{g}{first}", align_bytes=64)
             s = keep.tile([P, count * P], U8, name=f"scales{a}{g}{first}", align_bytes=64)
             nc.vector.quantize_mx(out=c[:].bitcast(FP8X4), scales=s[:], in_=woven[:].rearrange("p t m j -> p (t m j)"))
             for i in range(count):
@@ -168,11 +168,9 @@ def tile_picked_hub_silu_p_kernel(
         for t in range(2):
             for h in range(HALVES):
                 product_pass(0, 0, t, h)
-        wa = weave(0, 1, 0, 2, "vector", "wc")
-        wb = weave(0, 1, 2, 2, "scalar", "wd")
-        quantise(0, 0, 2, wb0)
-        quantise(0, 1, 0, wa)
-        quantise(0, 1, 2, wb)
+        quantise(0, 1, 0, weave(0, 1, 0, 2, "scalar", "wc"), "wf")
+        quantise(0, 0, 2, wb0, "wc")
+        quantise(0, 1, 2, weave(0, 1, 2, 2, "vector", "wb"))
         for t in range(2):
             for h in range(HALVES):
                 product_pass(0, 1, t, h)
@@ -223,40 +221,27 @@ def tile_picked_hub_silu_p_kernel(
         join(1, 0, U)
         activate(0, 0, U)
         join(2, 0, U)
-        starts = range(0, U, EDGE_SLICE)
-        for first in starts:
-            join(3, first, first + EDGE_SLICE)
-            activate(1, first, first + EDGE_SLICE)
+        for first, last in EDGE_SLICES:
+            join(3, first, last)
+            activate(1, first, last)
         zc, zs = {}, {}
-        for first in starts:
-            zc[first] = keep.tile([P, EDGE_SLICE], U32, name=f"zc{first}", align_bytes=64)
-            zs[first] = keep.tile([P, EDGE_SLICE], U8, name=f"zs{first}", align_bytes=64)
-            part = z[:, first : first + EDGE_SLICE, :].rearrange("p r t -> p (r t)")
+        for first, last in EDGE_SLICES:
+            zc[first] = keep.tile([P, last - first], U32, name=f"zc{first}", align_bytes=64)
+            zs[first] = keep.tile([P, last - first], U8, name=f"zs{first}", align_bytes=64)
+            part = z[:, first:last, :].rearrange("p r t -> p (r t)")
             nc.vector.quantize_mx(out=zc[first][:].bitcast(FP8X4), scales=zs[first][:], in_=part)
 
-        def last_product(acc, m, first):
-            cols = slice(m * P, (m + 1) * P)
-            nc.tensor.matmul_mx(
-                out=acc, lhsT=w3_c[:, cols].bitcast(FP8X4), lhsT_scale=w3_s[:, cols],
-                rhs=zc[first][:].bitcast(FP8X4), rhs_scale=zs[first][:], start=True, stop=True,
-            )
-
-        for i, first in enumerate(starts):
-            res = keep.tile([P, N // P, EDGE_SLICE], F32, name=f"res{first}", align_bytes=64)
-            if i < len(starts) - 1:
-                acc = psum.tile([P, N // P, EDGE_SLICE], F32, name=f"acc{first}", tag="bank")
-                for m in range(N // P):
-                    last_product(acc[:, m, :], m, first)
-                if i < 2:
-                    nc.scalar.copy(out=res[:], in_=acc[:])
-                else:
-                    nc.vector.tensor_copy(out=res[:], in_=acc[:])
+        for i, (first, last) in enumerate(EDGE_SLICES):
+            res = keep.tile([P, N // P, last - first], F32, name=f"res{first}", align_bytes=64)
+            acc = psum.tile([P, N // P, last - first], F32, name=f"acc{first}", tag="bank")
+            for m in range(N // P):
+                cols = slice(m * P, (m + 1) * P)
+                nc.tensor.matmul_mx(
+                    out=acc[:, m, :], lhsT=w3_c[:, cols].bitcast(FP8X4), lhsT_scale=w3_s[:, cols],
+                    rhs=zc[first][:].bitcast(FP8X4), rhs_scale=zs[first][:], start=True, stop=True,
+                )
+            if i in (2, 4):
+                nc.vector.tensor_copy(out=res[:], in_=acc[:])
             else:
-                for m in range(N // P):
-                    acc = psum.tile([P, EDGE_SLICE], F32, name=f"acc{first}{m}", tag="bank")
-                    last_product(acc[:], m, first)
-                    if m == 0:
-                        nc.scalar.copy(out=res[:, m, :], in_=acc[:])
-                    else:
-                        nc.vector.tensor_copy(out=res[:, m, :], in_=acc[:])
-            nc.sync.dma_start(out=out_v[:, :, first : first + EDGE_SLICE], in_=res[:])
+                nc.scalar.copy(out=res[:], in_=acc[:])
+            nc.sync.dma_start(out=out_v[:, :, first:last], in_=res[:])

@@ -17,16 +17,28 @@ SILU = mybir.ActivationFunctionType.Silu
 
 P = 128
 PACK = 4
+PAIR = 2
 K_PASS = P * PACK
 PASSES = K // K_PASS
 BANK = 512
+PSUM_BANKS = 8
 HALVES = S // BANK
 LIST_ROWS = 16
 QUADRANT = 32
 SCALE_ROWS = 4
-EDGE_SLICES = ((0, 256), (256, 512), (512, 768), (768, 896), (896, 1024))
+Y, E = 0, 1
+
 Y_WINDOW = 1376
 E_WINDOW = S + LIST_ROWS
+
+EDGE_SLICES = ((0, 256), (256, 512), (512, 768), (768, 896), (896, 1024))
+SLICES_ON_VECTOR = (2, 4)
+
+BUF_X1 = "wa"
+BUF_W1_LATE = "wb"
+BUF_W1_EARLY = "wc"
+BUF_W2_PASS0 = "wf"
+BUF_W2_PASS1 = "wh"
 
 
 def entries(list_tile, first, last):
@@ -37,10 +49,11 @@ def tile_picked_hub_silu_p_kernel(
     tc, x_words, x_scales, w1, w2, w3_words, w3_scales, offs, src, dst, out
 ):
     nc = tc.nc
+    on_scalar, on_vector = nc.scalar.copy, nc.vector.tensor_copy
     with ExitStack() as ctx:
         lists = ctx.enter_context(tc.tile_pool(name="lists", bufs=1))
         keep = ctx.enter_context(tc.tile_pool(name="keep", bufs=1))
-        psum = ctx.enter_context(tc.psum_pool(name="psum", bufs=8))
+        psum = ctx.enter_context(tc.psum_pool(name="psum", bufs=PSUM_BANKS))
 
         offs_t = lists.tile([P, S // LIST_ROWS], U16, name="offs_t")
         src_t = lists.tile([P, U // LIST_ROWS], U16, name="src_t")
@@ -49,14 +62,13 @@ def tile_picked_hub_silu_p_kernel(
         xs_all = keep.tile([P, T], U8, name="xs_all", align_bytes=64)
         w3_s = keep.tile([P, N], U8, name="w3_s", align_bytes=64)
         w3_c = keep.tile([P, N], U32, name="w3_c", align_bytes=64)
-        warm = keep.tile([P, 2], F32, name="warm")
         nc.vector.memset(xs_all[:].bitcast(I32), 0)
         nc.vector.memset(w3_s[:].bitcast(I32), 0)
 
         xw_all = [keep.tile([P, T], U32, name=f"xw_all{g}", align_bytes=64) for g in range(PASSES)]
         raw = {
             (a, g): keep.tile([P, PACK, H], F32, name=f"raw{a}{g}", align_bytes=64)
-            for a in range(2)
+            for a in (Y, E)
             for g in range(PASSES)
         }
 
@@ -66,8 +78,8 @@ def tile_picked_hub_silu_p_kernel(
             )
 
         def load_weight(a, g):
-            rows = (w1, w2)[a][g * K_PASS : (g + 1) * K_PASS, :]
-            nc.sync.dma_start(out=raw[a, g][:], in_=rows.rearrange("(p j) c -> p j c", j=PACK))
+            k_rows = (w1, w2)[a][g * K_PASS : (g + 1) * K_PASS, :]
+            nc.sync.dma_start(out=raw[a, g][:], in_=k_rows.rearrange("(p j) c -> p j c", j=PACK))
 
         nc.sync.dma_start(offs_t[:], offs)
         for q in range(P // QUADRANT):
@@ -75,13 +87,12 @@ def tile_picked_hub_silu_p_kernel(
                 out=xs_all[QUADRANT * q : QUADRANT * q + PASSES * SCALE_ROWS, :].bitcast(I32),
                 in_=x_scales[:, SCALE_ROWS * q : SCALE_ROWS * (q + 1), :].bitcast(I32),
             )
-        load_words(0)
-        load_weight(0, 0)
-        load_words(1)
-        load_weight(0, 1)
+        for g in range(PASSES):
+            load_words(g)
+            load_weight(Y, g)
         nc.sync.dma_start(src_t[:], src)
-        load_weight(1, 0)
-        load_weight(1, 1)
+        for g in range(PASSES):
+            load_weight(E, g)
         nc.sync.dma_start(dst_t[:], dst)
         nc.sync.dma_start(out=w3_c[:].bitcast(I32), in_=w3_words[0].rearrange("p n t -> p (n t)").bitcast(I32))
         for q in range(P // QUADRANT):
@@ -89,9 +100,6 @@ def tile_picked_hub_silu_p_kernel(
                 out=w3_s[QUADRANT * q : QUADRANT * q + SCALE_ROWS, :].bitcast(I32),
                 in_=w3_scales[0, SCALE_ROWS * q : SCALE_ROWS * (q + 1), :].bitcast(I32),
             )
-
-        nc.gpsimd.memset(warm[:, 0:1], 0.0)
-        nc.scalar.activation(out=warm[:, 1:2], in_=warm[:, 0:1], func=SILU)
 
         xs = keep.tile([P, S], U8, name="xs", align_bytes=64)
         xw = {}
@@ -101,24 +109,23 @@ def tile_picked_hub_silu_p_kernel(
             xw[g] = keep.tile([P, S], U32, name=f"xw{g}", tag=tag, align_bytes=64)
             nc.vector.tensor_copy(out=xw[g][:], in_=xw_all[g][:].indirect(offs_t[:]))
 
-        def weave(a, g, first, count, engine, tag):
+        def weave(a, g, first, count, copy, tag):
             woven = keep.tile([P, count, P, PACK], BF16, name=f"woven{a}{g}{first}", tag=tag, align_bytes=64)
-            o = woven[:].rearrange("p t m j -> p m j t")
-            i = raw[a, g][:].rearrange("p j (m t) -> p m j t", t=PACK)[:, :, :, first : first + count]
-            if engine == "scalar":
-                nc.scalar.copy(out=o, in_=i)
-            else:
-                nc.vector.tensor_copy(out=o, in_=i)
+            dealt = raw[a, g][:].rearrange("p j (m t) -> p m j t", t=PACK)[:, :, :, first : first + count]
+            copy(out=woven[:].rearrange("p t m j -> p m j t"), in_=dealt)
             return woven
 
         def quantise(a, g, first, woven, tag=None):
             count = woven.shape[1]
-            c = keep.tile([P, count * P], U32, name=f"codes{a}{g}{first}", tag=tag or f"codes{a}{g}{first}", align_bytes=64)
-            s = keep.tile([P, count * P], U8, name=f"scales{a}{g}{first}", align_bytes=64)
-            nc.vector.quantize_mx(out=c[:].bitcast(FP8X4), scales=s[:], in_=woven[:].rearrange("p t m j -> p (t m j)"))
-            for i in range(count):
-                codes[a, g, first + i] = c[:, i * P : (i + 1) * P]
-                scales[a, g, first + i] = s[:, i * P : (i + 1) * P]
+            name = f"codes{a}{g}{first}"
+            words = keep.tile([P, count * P], U32, name=name, tag=tag or name, align_bytes=64)
+            plane = keep.tile([P, count * P], U8, name=f"scales{a}{g}{first}", align_bytes=64)
+            nc.vector.quantize_mx(
+                out=words[:].bitcast(FP8X4), scales=plane[:], in_=woven[:].rearrange("p t m j -> p (t m j)")
+            )
+            for n in range(count):
+                codes[a, g, first + n] = words[:, n * P : (n + 1) * P]
+                scales[a, g, first + n] = plane[:, n * P : (n + 1) * P]
 
         banks = {}
 
@@ -138,67 +145,63 @@ def tile_picked_hub_silu_p_kernel(
 
         y_all = keep.tile([P, (PACK - 1) * S + Y_WINDOW], F32, name="y_all", align_bytes=64)
         nc.gpsimd.memset(y_all[:, PACK * S :], 0.0)
-        e_all = [keep.tile([P, E_WINDOW if t < PACK - 1 else S], F32, name=f"e_all{t}", align_bytes=64) for t in range(PACK)]
+        e_all = [
+            keep.tile([P, E_WINDOW if t < PACK - 1 else S], F32, name=f"e_all{t}", align_bytes=64) for t in range(PACK)
+        ]
         for t in range(PACK - 1):
             nc.gpsimd.memset(e_all[t][:, S:], 0.0)
-        rows = {(0, t): y_all[:, (PACK - 1 - t) * S : (PACK - t) * S] for t in range(PACK)}
-        rows.update({(1, t): e_all[t][:, :S] for t in range(PACK)})
+        y_start = [(PACK - 1 - t) * S for t in range(PACK)]
+        results = {(Y, t): y_all[:, y_start[t] : y_start[t] + S] for t in range(PACK)}
+        results.update({(E, t): e_all[t][:, :S] for t in range(PACK)})
 
-        def empty_bank(a, t, h, engine="scalar"):
-            o = rows[a, t][:, h * BANK : (h + 1) * BANK]
-            if engine == "scalar":
-                nc.scalar.copy(out=o, in_=banks[a, t, h][:])
-            else:
-                nc.vector.tensor_copy(out=o, in_=banks[a, t, h][:])
+        def empty_bank(a, t, h, copy=on_scalar):
+            copy(out=results[a, t][:, h * BANK : (h + 1) * BANK], in_=banks[a, t, h][:])
 
         fetched = {}
 
         def fetch_sources(t, tag):
             fetched[t] = keep.tile([P, U], F32, name=f"fetched{t}", tag=tag, align_bytes=64)
-            at = (PACK - 1 - t) * S
-            nc.vector.tensor_copy(out=fetched[t][:], in_=y_all[:, at : at + Y_WINDOW].indirect(src_t[:]))
+            window = y_all[:, y_start[t] : y_start[t] + Y_WINDOW]
+            nc.vector.tensor_copy(out=fetched[t][:], in_=window.indirect(src_t[:]))
 
         nc.vector.tensor_copy(out=xs[:], in_=xs_all[:].indirect(offs_t[:]))
         gather_words(0, "xw0")
-        wa = weave(0, 0, 0, 2, "scalar", "wa")
-        wb = weave(0, 0, 2, 2, "scalar", "wb")
-        quantise(0, 0, 0, wa)
-        gather_words(1, "wa")
-        wb0 = wb
-        for t in range(2):
+        early_pass0 = weave(Y, 0, 0, PAIR, on_scalar, BUF_X1)
+        late_pass0 = weave(Y, 0, PAIR, PAIR, on_scalar, BUF_W1_LATE)
+        quantise(Y, 0, 0, early_pass0)
+        gather_words(1, BUF_X1)
+        for t in range(PAIR):
             for h in range(HALVES):
-                product_pass(0, 0, t, h)
-        quantise(0, 1, 0, weave(0, 1, 0, 2, "scalar", "wc"), "wf")
-        quantise(0, 0, 2, wb0, "wc")
-        quantise(0, 1, 2, weave(0, 1, 2, 2, "vector", "wb"))
-        for t in range(2):
+                product_pass(Y, 0, t, h)
+        quantise(Y, 1, 0, weave(Y, 1, 0, PAIR, on_scalar, BUF_W1_EARLY), BUF_W2_PASS0)
+        quantise(Y, 0, PAIR, late_pass0, BUF_W1_EARLY)
+        quantise(Y, 1, PAIR, weave(Y, 1, PAIR, PAIR, on_vector, BUF_W1_LATE))
+        for t in range(PAIR):
             for h in range(HALVES):
-                product_pass(0, 1, t, h)
-        for t in range(2, PACK):
+                product_pass(Y, 1, t, h)
+        for t in range(PAIR, PACK):
             for h in range(HALVES):
                 for g in range(PASSES):
-                    product_pass(0, g, t, h)
-        empty_bank(0, 0, 0)
-        empty_bank(0, 0, 1, "vector")
+                    product_pass(Y, g, t, h)
+
+        empty_bank(Y, 0, 0)
+        empty_bank(Y, 0, 1, on_vector)
         fetch_sources(0, "f0")
-        empty_bank(0, 1, 0)
-        empty_bank(0, 1, 1)
+        for h in range(HALVES):
+            empty_bank(Y, 1, h)
         fetch_sources(1, "f1")
-        wa = weave(1, 0, 0, PACK, "scalar", "wf")
-        empty_bank(0, 2, 0)
-        empty_bank(0, 2, 1)
-        quantise(1, 0, 0, wa)
-        fetch_sources(2, "wf")
-        wa = weave(1, 1, 0, PACK, "scalar", "wh")
-        empty_bank(0, 3, 0)
-        empty_bank(0, 3, 1)
-        quantise(1, 1, 0, wa)
-        fetch_sources(3, "wh")
+        for g, tag in enumerate((BUF_W2_PASS0, BUF_W2_PASS1)):
+            woven_w2 = weave(E, g, 0, PACK, on_scalar, tag)
+            for h in range(HALVES):
+                empty_bank(Y, PAIR + g, h)
+            quantise(E, g, 0, woven_w2)
+            fetch_sources(PAIR + g, tag)
+
         for t in range(PACK):
             for h in range(HALVES):
                 for g in range(PASSES):
-                    product_pass(1, g, t, h)
-                empty_bank(1, t, h)
+                    product_pass(E, g, t, h)
+                empty_bank(E, t, h)
 
         out_v = out.rearrange("(mt p) r -> p mt r", p=P)
 
@@ -207,13 +210,16 @@ def tile_picked_hub_silu_p_kernel(
 
         def join(t, first, last):
             nc.vector.tensor_tensor(
-                out=u[:, t, first:last], in0=e_all[t][:].indirect(entries(dst_t, first, last)), in1=fetched[t][:, first:last], op=ADD
+                out=u[:, t, first:last],
+                in0=e_all[t][:].indirect(entries(dst_t, first, last)),
+                in1=fetched[t][:, first:last],
+                op=ADD,
             )
 
-        def activate(pair, first, last):
+        def activate(t, first, last):
             nc.scalar.activation(
-                out=z[:, first:last, 2 * pair : 2 * pair + 2],
-                in_=u[:, 2 * pair : 2 * pair + 2, first:last].rearrange("p t r -> p r t"),
+                out=z[:, first:last, t : t + PAIR],
+                in_=u[:, t : t + PAIR, first:last].rearrange("p t r -> p r t"),
                 func=SILU,
             )
 
@@ -223,25 +229,31 @@ def tile_picked_hub_silu_p_kernel(
         join(2, 0, U)
         for first, last in EDGE_SLICES:
             join(3, first, last)
-            activate(1, first, last)
-        zc, zs = {}, {}
+            activate(PAIR, first, last)
+        z_words, z_scales = {}, {}
         for first, last in EDGE_SLICES:
-            zc[first] = keep.tile([P, last - first], U32, name=f"zc{first}", align_bytes=64)
-            zs[first] = keep.tile([P, last - first], U8, name=f"zs{first}", align_bytes=64)
-            part = z[:, first:last, :].rearrange("p r t -> p (r t)")
-            nc.vector.quantize_mx(out=zc[first][:].bitcast(FP8X4), scales=zs[first][:], in_=part)
+            z_words[first] = keep.tile([P, last - first], U32, name=f"zc{first}", align_bytes=64)
+            z_scales[first] = keep.tile([P, last - first], U8, name=f"zs{first}", align_bytes=64)
+            nc.vector.quantize_mx(
+                out=z_words[first][:].bitcast(FP8X4),
+                scales=z_scales[first][:],
+                in_=z[:, first:last, :].rearrange("p r t -> p (r t)"),
+            )
 
-        for i, (first, last) in enumerate(EDGE_SLICES):
+        for number, (first, last) in enumerate(EDGE_SLICES):
             res = keep.tile([P, N // P, last - first], F32, name=f"res{first}", align_bytes=64)
             acc = psum.tile([P, N // P, last - first], F32, name=f"acc{first}", tag="bank")
-            for m in range(N // P):
-                cols = slice(m * P, (m + 1) * P)
+            for block in range(N // P):
+                cols = slice(block * P, (block + 1) * P)
                 nc.tensor.matmul_mx(
-                    out=acc[:, m, :], lhsT=w3_c[:, cols].bitcast(FP8X4), lhsT_scale=w3_s[:, cols],
-                    rhs=zc[first][:].bitcast(FP8X4), rhs_scale=zs[first][:], start=True, stop=True,
+                    out=acc[:, block, :],
+                    lhsT=w3_c[:, cols].bitcast(FP8X4),
+                    lhsT_scale=w3_s[:, cols],
+                    rhs=z_words[first][:].bitcast(FP8X4),
+                    rhs_scale=z_scales[first][:],
+                    start=True,
+                    stop=True,
                 )
-            if i in (2, 4):
-                nc.vector.tensor_copy(out=res[:], in_=acc[:])
-            else:
-                nc.scalar.copy(out=res[:], in_=acc[:])
+            copy = on_vector if number in SLICES_ON_VECTOR else on_scalar
+            copy(out=res[:], in_=acc[:])
             nc.sync.dma_start(out=out_v[:, :, first:last], in_=res[:])

@@ -31,14 +31,10 @@ Y, E = 0, 1
 Y_WINDOW = 1376
 E_WINDOW = S + LIST_ROWS
 
-EDGE_SLICES = ((0, 256), (256, 512), (512, 768), (768, 896), (896, 1024))
-SLICES_ON_VECTOR = (2, 4)
+EDGE_SLICES = ((128,),(256,256,),(256,),(128,),)
 
-BUF_X1 = "wa"
-BUF_W1_LATE = "wb"
-BUF_W1_EARLY = "wc"
-BUF_W2_PASS0 = "wf"
-BUF_W2_PASS1 = "wh"
+WEAVE_ON_SCALAR = 64
+BANK_PAIRS = ((0, 1, 2, 0), (3, 1, 2, 0))
 
 
 def entries(list_tile, first, last):
@@ -53,7 +49,7 @@ def tile_picked_hub_silu_p_kernel(
     with ExitStack() as ctx:
         lists = ctx.enter_context(tc.tile_pool(name="lists", bufs=1))
         keep = ctx.enter_context(tc.tile_pool(name="keep", bufs=1))
-        psum = ctx.enter_context(tc.psum_pool(name="psum", bufs=PSUM_BANKS))
+        psum = ctx.enter_context(tc.psum_pool(name="psum", bufs=1))
 
         offs_t = lists.tile([P, S // LIST_ROWS], U16, name="offs_t")
         src_t = lists.tile([P, U // LIST_ROWS], U16, name="src_t")
@@ -63,9 +59,9 @@ def tile_picked_hub_silu_p_kernel(
         w3_s = keep.tile([P, N], U8, name="w3_s", align_bytes=64)
         w3_c = keep.tile([P, N], U32, name="w3_c", align_bytes=64)
         nc.vector.memset(xs_all[:].bitcast(I32), 0)
-        nc.vector.memset(w3_s[:].bitcast(I32), 0)
+        nc.gpsimd.memset(w3_s[:].bitcast(I32), 0)
 
-        xw_all = [keep.tile([P, T], U32, name=f"xw_all{g}", align_bytes=64) for g in range(PASSES)]
+        xw_all = [keep.tile([P, T], U32, name=f"xw_all{g}", tag=f"xw_all{g}", align_bytes=64) for g in range(PASSES)]
         raw = {
             (a, g): keep.tile([P, PACK, H], F32, name=f"raw{a}{g}", align_bytes=64)
             for a in (Y, E)
@@ -81,15 +77,16 @@ def tile_picked_hub_silu_p_kernel(
             k_rows = (w1, w2)[a][g * K_PASS : (g + 1) * K_PASS, :]
             nc.sync.dma_start(out=raw[a, g][:], in_=k_rows.rearrange("(p j) c -> p j c", j=PACK))
 
+        load_words(0)
         nc.sync.dma_start(offs_t[:], offs)
         for q in range(P // QUADRANT):
             nc.sync.dma_start(
                 out=xs_all[QUADRANT * q : QUADRANT * q + PASSES * SCALE_ROWS, :].bitcast(I32),
                 in_=x_scales[:, SCALE_ROWS * q : SCALE_ROWS * (q + 1), :].bitcast(I32),
             )
-        for g in range(PASSES):
-            load_words(g)
-            load_weight(Y, g)
+        load_weight(Y, 0)
+        load_words(1)
+        load_weight(Y, 1)
         nc.sync.dma_start(src_t[:], src)
         for g in range(PASSES):
             load_weight(E, g)
@@ -109,11 +106,13 @@ def tile_picked_hub_silu_p_kernel(
             xw[g] = keep.tile([P, S], U32, name=f"xw{g}", tag=tag, align_bytes=64)
             nc.vector.tensor_copy(out=xw[g][:], in_=xw_all[g][:].indirect(offs_t[:]))
 
-        def weave(a, g, first, count, copy, tag):
-            woven = keep.tile([P, count, P, PACK], BF16, name=f"woven{a}{g}{first}", tag=tag, align_bytes=64)
-            dealt = raw[a, g][:].rearrange("p j (m t) -> p m j t", t=PACK)[:, :, :, first : first + count]
-            copy(out=woven[:].rearrange("p t m j -> p m j t"), in_=dealt)
-            return woven
+        def woven_tile(a, g, first, count, tag=None):
+            name = f"woven{a}{g}{first}"
+            return keep.tile([P, count, P, PACK], BF16, name=name, tag=tag or name, align_bytes=64)
+
+        def weave(a, g, first, copy, woven):
+            dealt = raw[a, g][:].rearrange("p j (m t) -> p m j t", t=PACK)[:, :, :, first : first + PAIR]
+            copy(out=woven.rearrange("p t m j -> p m j t"), in_=dealt)
 
         def quantise(a, g, first, woven, tag=None):
             count = woven.shape[1]
@@ -127,11 +126,24 @@ def tile_picked_hub_silu_p_kernel(
                 codes[a, g, first + n] = words[:, n * P : (n + 1) * P]
                 scales[a, g, first + n] = plane[:, n * P : (n + 1) * P]
 
+        def woven_pair(a, g, first, copy, tag=None):
+            woven = woven_tile(a, g, first, PAIR, tag)
+            weave(a, g, first, copy, woven[:])
+            return woven
+
+        def woven_shared(first, on_scalar_columns, tag=None):
+            woven = woven_tile(Y, 1, first, PAIR, tag)
+            dealt = raw[Y, 1][:].rearrange("p j (m t) -> p m j t", t=PACK)[:, :, :, first : first + PAIR]
+            laid = woven[:].rearrange("p t m j -> p m j t")
+            on_scalar(out=laid[:, :on_scalar_columns], in_=dealt[:, :on_scalar_columns])
+            on_vector(out=laid[:, on_scalar_columns:], in_=dealt[:, on_scalar_columns:])
+            return woven
+
         banks = {}
 
         def product_pass(a, g, t, h):
             if g == 0:
-                banks[a, t, h] = psum.tile([P, BANK], F32, name=f"bank{a}{t}{h}", tag="bank")
+                banks[a, t, h] = psum.tile([P, BANK], F32, name=f"bank{a}{t}{h}", tag=f"bank{BANK_PAIRS[a][t]}{h}")
             picked = slice(h * BANK, (h + 1) * BANK)
             nc.tensor.matmul_mx(
                 out=banks[a, t, h][:],
@@ -143,13 +155,31 @@ def tile_picked_hub_silu_p_kernel(
                 stop=(g == PASSES - 1),
             )
 
+        quarters = [psum.tile([P, BANK // 2], F32, name=f"quarter{n}", tag=f"bank{(0, 3)[n // 2]}{n % 2}") for n in range(4)]
+
+        def first_tile_pass(g):
+            for n in range(4):
+                picked = slice(n * BANK // 2, (n + 1) * BANK // 2)
+                nc.tensor.matmul_mx(
+                    out=quarters[n][:],
+                    lhsT=codes[Y, g, 0].bitcast(FP8X4),
+                    lhsT_scale=scales[Y, g, 0],
+                    rhs=xw[g][:, picked].bitcast(FP8X4),
+                    rhs_scale=xs[SCALE_ROWS * g :, picked],
+                    start=(g == 0),
+                    stop=(g == PASSES - 1),
+                )
+
+        def product_pair(a, g, first):
+            for t in range(first, first + PAIR):
+                for h in range(HALVES):
+                    product_pass(a, g, t, h)
+
         y_all = keep.tile([P, (PACK - 1) * S + Y_WINDOW], F32, name="y_all", align_bytes=64)
         nc.gpsimd.memset(y_all[:, PACK * S :], 0.0)
-        e_all = [
-            keep.tile([P, E_WINDOW if t < PACK - 1 else S], F32, name=f"e_all{t}", align_bytes=64) for t in range(PACK)
-        ]
-        for t in range(PACK - 1):
-            nc.gpsimd.memset(e_all[t][:, S:], 0.0)
+        warm = keep.tile([P, 1], F32, name="warm")
+        nc.scalar.activation(out=warm[:], in_=y_all[:, PACK * S : PACK * S + 1], func=SILU)
+        e_all = [keep.tile([P, S], F32, name=f"e_all{t}", align_bytes=64) for t in range(PACK)]
         y_start = [(PACK - 1 - t) * S for t in range(PACK)]
         results = {(Y, t): y_all[:, y_start[t] : y_start[t] + S] for t in range(PACK)}
         results.update({(E, t): e_all[t][:, :S] for t in range(PACK)})
@@ -157,103 +187,109 @@ def tile_picked_hub_silu_p_kernel(
         def empty_bank(a, t, h, copy=on_scalar):
             copy(out=results[a, t][:, h * BANK : (h + 1) * BANK], in_=banks[a, t, h][:])
 
-        fetched = {}
+        def empty_tile(a, t):
+            for h in range(HALVES):
+                empty_bank(a, t, h)
 
-        def fetch_sources(t, tag):
-            fetched[t] = keep.tile([P, U], F32, name=f"fetched{t}", tag=tag, align_bytes=64)
+        fetched = [keep.tile([P, U], F32, name=f"fetched{t}", align_bytes=64) for t in range(PACK)]
+
+        def fetch_sources(t):
             window = y_all[:, y_start[t] : y_start[t] + Y_WINDOW]
             nc.vector.tensor_copy(out=fetched[t][:], in_=window.indirect(src_t[:]))
 
-        nc.vector.tensor_copy(out=xs[:], in_=xs_all[:].indirect(offs_t[:]))
         gather_words(0, "xw0")
-        early_pass0 = weave(Y, 0, 0, PAIR, on_scalar, BUF_X1)
-        late_pass0 = weave(Y, 0, PAIR, PAIR, on_scalar, BUF_W1_LATE)
-        quantise(Y, 0, 0, early_pass0)
-        gather_words(1, BUF_X1)
-        for t in range(PAIR):
-            for h in range(HALVES):
-                product_pass(Y, 0, t, h)
-        quantise(Y, 1, 0, weave(Y, 1, 0, PAIR, on_scalar, BUF_W1_EARLY), BUF_W2_PASS0)
-        quantise(Y, 0, PAIR, late_pass0, BUF_W1_EARLY)
-        quantise(Y, 1, PAIR, weave(Y, 1, PAIR, PAIR, on_vector, BUF_W1_LATE))
-        for t in range(PAIR):
-            for h in range(HALVES):
-                product_pass(Y, 1, t, h)
-        for t in range(PAIR, PACK):
-            for h in range(HALVES):
-                for g in range(PASSES):
-                    product_pass(Y, g, t, h)
-
-        empty_bank(Y, 0, 0)
-        empty_bank(Y, 0, 1, on_vector)
-        fetch_sources(0, "f0")
+        nc.vector.tensor_copy(out=xs[:], in_=xs_all[:].indirect(offs_t[:]))
+        quantise(Y, 0, 0, woven_pair(Y, 0, 0, on_scalar))
+        late = woven_pair(Y, 0, PAIR, on_scalar)
+        gather_words(1, "xw1")
+        first_tile_pass(0)
         for h in range(HALVES):
-            empty_bank(Y, 1, h)
-        fetch_sources(1, "f1")
-        for g, tag in enumerate((BUF_W2_PASS0, BUF_W2_PASS1)):
-            woven_w2 = weave(E, g, 0, PACK, on_scalar, tag)
-            for h in range(HALVES):
-                empty_bank(Y, PAIR + g, h)
-            quantise(E, g, 0, woven_w2)
-            fetch_sources(PAIR + g, tag)
+            product_pass(Y, 0, 1, h)
+        quantise(Y, 1, 0, woven_shared(0, 72))
+        first_tile_pass(1)
+        for h in range(HALVES):
+            product_pass(Y, 1, 1, h)
+        quantise(Y, 0, PAIR, late, "woven010")
+        late_pass1 = woven_shared(PAIR, 96)
 
+        for n in range(4):
+            copy = (on_scalar, on_vector)[n % 2]
+            copy(out=results[Y, 0][:, n * BANK // 2 : (n + 1) * BANK // 2], in_=quarters[n][:])
+        quantise(Y, 1, PAIR, late_pass1, "woven002")
+        for h in range(HALVES):
+            for g in range(PASSES):
+                product_pass(Y, g, PAIR, h)
+        fetch_sources(0)
+        for h in range(HALVES):
+            for g in range(PASSES):
+                product_pass(Y, g, PACK - 1, h)
+        empty_tile(Y, 1)
+        fetch_sources(1)
+        for g in range(PASSES):
+            quantise(E, g, 0, woven_pair(E, g, 0, on_scalar, ("codes010", "scales010")[g]))
+            product_pair(E, g, 0)
+        for g in range(PASSES):
+            empty_tile(Y, PAIR + g) if g == 0 else None
+            woven = woven_pair(E, g, PAIR, on_scalar, ("woven002", "scales012")[g])
+            if g == 0:
+                fetch_sources(PAIR)
+            quantise(E, g, PAIR, woven)
+            product_pair(E, g, PAIR)
+            if g == 0:
+                empty_tile(Y, PAIR + 1)
+                fetch_sources(PAIR + 1)
         for t in range(PACK):
-            for h in range(HALVES):
-                for g in range(PASSES):
-                    product_pass(E, g, t, h)
-                empty_bank(E, t, h)
+            empty_tile(E, t)
 
         out_v = out.rearrange("(mt p) r -> p mt r", p=P)
+        ring = ctx.enter_context(tc.tile_pool(name="ring", bufs=2))
 
-        u = keep.tile([P, PACK, U], F32, name="u", align_bytes=64)
-        z = keep.tile([P, U, PACK], BF16, name="z", align_bytes=64)
+        def finish(first, widths, z, copy=on_scalar):
+            start = first
+            for width in widths:
+                last = first + width
+                z_words = keep.tile([P, width], U32, name=f"zc{first}", align_bytes=64)
+                z_scales = keep.tile([P, width], U8, name=f"zs{first}", align_bytes=64)
+                values = z[:, (first - start) * PACK : (last - start) * PACK]
+                nc.vector.quantize_mx(out=z_words[:].bitcast(FP8X4), scales=z_scales[:], in_=values)
+                res = keep.tile([P, N // P, width], F32, name=f"res{first}", align_bytes=64)
+                bank = "bank%d%d" % divmod((len(done) + 6) % PSUM_BANKS, HALVES)
+                done.append(first)
+                acc = psum.tile([P, N // P, width], F32, name=f"acc{first}", tag=bank)
+                for block in range(N // P):
+                    cols = slice(block * P, (block + 1) * P)
+                    nc.tensor.matmul_mx(
+                        out=acc[:, block, :],
+                        lhsT=w3_c[:, cols].bitcast(FP8X4),
+                        lhsT_scale=w3_s[:, cols],
+                        rhs=z_words[:].bitcast(FP8X4),
+                        rhs_scale=z_scales[:],
+                        start=True,
+                        stop=True,
+                    )
+                copy(out=res[:], in_=acc[:])
+                nc.sync.dma_start(out=out_v[:, :, first:last], in_=res[:])
+                first = last
 
-        def join(t, first, last):
-            nc.vector.tensor_tensor(
-                out=u[:, t, first:last],
-                in0=e_all[t][:].indirect(entries(dst_t, first, last)),
-                in1=fetched[t][:, first:last],
-                op=ADD,
-            )
-
-        def activate(t, first, last):
+        done, waiting, first = [], None, 0
+        for widths in EDGE_SLICES:
+            last = first + sum(widths)
+            u = ring.tile([P, PACK, last - first], F32, name=f"u{first}", tag="u", align_bytes=64)
+            for t in range(PACK):
+                nc.vector.tensor_tensor(
+                    out=u[:, t, :],
+                    in0=e_all[t][:].indirect(entries(dst_t, first, last)),
+                    in1=fetched[t][:, first:last],
+                    op=ADD,
+                )
+            z = keep.tile([P, (last - first) * PACK], BF16, name=f"z{first}", align_bytes=64)
             nc.scalar.activation(
-                out=z[:, first:last, t : t + PAIR],
-                in_=u[:, t : t + PAIR, first:last].rearrange("p t r -> p r t"),
+                out=z[:].rearrange("p (c i t) -> p c t i", i=PACK, t=PACK),
+                in_=u[:].rearrange("p t (c i) -> p c t i", i=PACK),
                 func=SILU,
             )
-
-        join(0, 0, U)
-        join(1, 0, U)
-        activate(0, 0, U)
-        join(2, 0, U)
-        for first, last in EDGE_SLICES:
-            join(3, first, last)
-            activate(PAIR, first, last)
-        z_words, z_scales = {}, {}
-        for first, last in EDGE_SLICES:
-            z_words[first] = keep.tile([P, last - first], U32, name=f"zc{first}", align_bytes=64)
-            z_scales[first] = keep.tile([P, last - first], U8, name=f"zs{first}", align_bytes=64)
-            nc.vector.quantize_mx(
-                out=z_words[first][:].bitcast(FP8X4),
-                scales=z_scales[first][:],
-                in_=z[:, first:last, :].rearrange("p r t -> p (r t)"),
-            )
-
-        for number, (first, last) in enumerate(EDGE_SLICES):
-            res = keep.tile([P, N // P, last - first], F32, name=f"res{first}", align_bytes=64)
-            acc = psum.tile([P, N // P, last - first], F32, name=f"acc{first}", tag="bank")
-            for block in range(N // P):
-                cols = slice(block * P, (block + 1) * P)
-                nc.tensor.matmul_mx(
-                    out=acc[:, block, :],
-                    lhsT=w3_c[:, cols].bitcast(FP8X4),
-                    lhsT_scale=w3_s[:, cols],
-                    rhs=z_words[first][:].bitcast(FP8X4),
-                    rhs_scale=z_scales[first][:],
-                    start=True,
-                    stop=True,
-                )
-            copy = on_vector if number in SLICES_ON_VECTOR else on_scalar
-            copy(out=res[:], in_=acc[:])
-            nc.sync.dma_start(out=out_v[:, :, first:last], in_=res[:])
+            if waiting:
+                finish(*waiting)
+            waiting = first, widths, z
+            first = last
+        finish(*waiting, on_vector)

@@ -33,7 +33,7 @@ E_WINDOW = S + LIST_ROWS
 
 EDGE_SLICES = ((128,),(256,256,),(256,),(128,),)
 
-WEAVE_ON_SCALAR = 64
+LATE_PIECES = ((0, 96), (96, 128))
 BANK_PAIRS = ((0, 1, 2, 0), (3, 1, 2, 0))
 
 
@@ -66,6 +66,7 @@ def tile_picked_hub_silu_p_kernel(
             (a, g): keep.tile([P, PACK, H], F32, name=f"raw{a}{g}", align_bytes=64)
             for a in (Y, E)
             for g in range(PASSES)
+            if (a, g) != (Y, 1)
         }
 
         def load_words(g):
@@ -86,7 +87,10 @@ def tile_picked_hub_silu_p_kernel(
             )
         load_weight(Y, 0)
         load_words(1)
-        load_weight(Y, 1)
+        late_rows = w1[K_PASS:, :].rearrange("(p j) c -> p j c", j=PACK)
+        late = [keep.tile([P, PACK, PACK * (m1 - m0)], F32, name=f"late{m0}", align_bytes=64) for m0, m1 in LATE_PIECES]
+        for tile, (m0, m1) in zip(late, LATE_PIECES):
+            nc.sync.dma_start(out=tile[:], in_=late_rows[:, :, PACK * m0 : PACK * m1])
         nc.sync.dma_start(src_t[:], src)
         for g in range(PASSES):
             load_weight(E, g)
@@ -131,12 +135,12 @@ def tile_picked_hub_silu_p_kernel(
             weave(a, g, first, copy, woven[:])
             return woven
 
-        def woven_shared(first, on_scalar_columns, tag=None):
-            woven = woven_tile(Y, 1, first, PAIR, tag)
-            dealt = raw[Y, 1][:].rearrange("p j (m t) -> p m j t", t=PACK)[:, :, :, first : first + PAIR]
+        def woven_late(first, copies):
+            woven = woven_tile(Y, 1, first, PAIR)
             laid = woven[:].rearrange("p t m j -> p m j t")
-            on_scalar(out=laid[:, :on_scalar_columns], in_=dealt[:, :on_scalar_columns])
-            on_vector(out=laid[:, on_scalar_columns:], in_=dealt[:, on_scalar_columns:])
+            for tile, (m0, m1), copy in zip(late, LATE_PIECES, copies):
+                dealt = tile[:].rearrange("p j (m t) -> p m j t", t=PACK)[:, :, :, first : first + PAIR]
+                copy(out=laid[:, m0:m1], in_=dealt)
             return woven
 
         banks = {}
@@ -200,17 +204,17 @@ def tile_picked_hub_silu_p_kernel(
         gather_words(0, "xw0")
         nc.vector.tensor_copy(out=xs[:], in_=xs_all[:].indirect(offs_t[:]))
         quantise(Y, 0, 0, woven_pair(Y, 0, 0, on_scalar))
-        late = woven_pair(Y, 0, PAIR, on_scalar)
+        late_pass0 = woven_pair(Y, 0, PAIR, on_scalar)
         gather_words(1, "xw1")
         first_tile_pass(0)
         for h in range(HALVES):
             product_pass(Y, 0, 1, h)
-        quantise(Y, 1, 0, woven_shared(0, 72))
+        quantise(Y, 1, 0, woven_late(0, (on_scalar, on_scalar)))
         first_tile_pass(1)
         for h in range(HALVES):
             product_pass(Y, 1, 1, h)
-        quantise(Y, 0, PAIR, late, "woven010")
-        late_pass1 = woven_shared(PAIR, 96)
+        quantise(Y, 0, PAIR, late_pass0, "woven010")
+        late_pass1 = woven_late(PAIR, (on_scalar, on_vector))
 
         for n in range(4):
             copy = (on_scalar, on_vector)[n % 2]
@@ -283,11 +287,14 @@ def tile_picked_hub_silu_p_kernel(
                     op=ADD,
                 )
             z = keep.tile([P, (last - first) * PACK], BF16, name=f"z{first}", align_bytes=64)
-            nc.scalar.activation(
-                out=z[:].rearrange("p (c i t) -> p c t i", i=PACK, t=PACK),
-                in_=u[:].rearrange("p t (c i) -> p c t i", i=PACK),
-                func=SILU,
-            )
+            at = 0
+            for width in widths:
+                nc.scalar.activation(
+                    out=z[:, at * PACK : (at + width) * PACK].rearrange("p (c i t) -> p c t i", i=PACK, t=PACK),
+                    in_=u[:, :, at : at + width].rearrange("p t (c i) -> p c t i", i=PACK),
+                    func=SILU,
+                )
+                at += width
             if waiting:
                 finish(*waiting)
             waiting = first, widths, z

@@ -229,20 +229,22 @@ def tile_picked_hub_silu_p_kernel(
                 product_pass(Y, g, PACK - 1, h)
         empty_tile(Y, 1)
         fetch_sources(1)
+        quantise(E, 0, 0, woven_pair(E, 0, 0, on_scalar, "codes010"))
+        empty_tile(Y, 2)
+        fetch_sources(2)
+        quantise(E, 1, 0, woven_pair(E, 1, 0, on_scalar, "scales010"))
+        empty_tile(Y, 3)
+        fetch_sources(3)
+        woven = woven_tile(E, 0, PAIR, PASSES * PAIR, "woven002")
         for g in range(PASSES):
-            quantise(E, g, 0, woven_pair(E, g, 0, on_scalar, ("codes010", "scales010")[g]))
-            product_pair(E, g, 0)
-        for g in range(PASSES):
-            empty_tile(Y, PAIR + g) if g == 0 else None
-            woven = woven_pair(E, g, PAIR, on_scalar, ("woven002", "scales012")[g])
-            if g == 0:
-                fetch_sources(PAIR)
-            quantise(E, g, PAIR, woven)
-            product_pair(E, g, PAIR)
-            if g == 0:
-                empty_tile(Y, PAIR + 1)
-                fetch_sources(PAIR + 1)
+            weave(E, g, PAIR, on_scalar, woven[:, PAIR * g : PAIR * (g + 1)])
+        quantise(E, 0, PAIR, woven)
+        for n in range(PAIR):
+            codes[E, 1, PAIR + n], scales[E, 1, PAIR + n] = codes[E, 0, PACK + n], scales[E, 0, PACK + n]
         for t in range(PACK):
+            for h in range(HALVES):
+                for g in range(PASSES):
+                    product_pass(E, g, t, h)
             empty_tile(E, t)
 
         out_v = out.rearrange("(mt p) r -> p mt r", p=P)
@@ -275,20 +277,24 @@ def tile_picked_hub_silu_p_kernel(
                 nc.sync.dma_start(out=out_v[:, :, first:last], in_=res[:])
                 first = last
 
+        def join(u, t, start, first, last):
+            nc.vector.tensor_tensor(
+                out=u[:, t, first - start : last - start],
+                in0=e_all[t][:].indirect(entries(dst_t, first, last)),
+                in1=fetched[t][:, first:last],
+                op=ADD,
+            )
+
         done, waiting, first = [], None, 0
         for widths in EDGE_SLICES:
             last = first + sum(widths)
             u = ring.tile([P, PACK, last - first], F32, name=f"u{first}", tag="u", align_bytes=64)
-            for t in range(PACK):
-                nc.vector.tensor_tensor(
-                    out=u[:, t, :],
-                    in0=e_all[t][:].indirect(entries(dst_t, first, last)),
-                    in1=fetched[t][:, first:last],
-                    op=ADD,
-                )
+            for t in range(PACK - 1):
+                join(u, t, first, first, last)
             z = keep.tile([P, (last - first) * PACK], BF16, name=f"z{first}", align_bytes=64)
             at = 0
             for width in widths:
+                join(u, PACK - 1, first, first + at, first + at + width)
                 nc.scalar.activation(
                     out=z[:, at * PACK : (at + width) * PACK].rearrange("p (c i t) -> p c t i", i=PACK, t=PACK),
                     in_=u[:, :, at : at + width].rearrange("p t (c i) -> p c t i", i=PACK),

@@ -34,7 +34,7 @@ E_WINDOW = S + LIST_ROWS
 EDGE_SLICES = ((128,),(256,256,),(256,),(128,),)
 
 LATE_PIECES = ((0, 96), (96, 128))
-BANK_PAIRS = ((0, 1, 2, 0), (3, 1, 2, 0))
+TILE_BANKS = ((None, (2, 3), (0, 1), (6, 7)), ((4, 5), (2, 3), (0, 1), (6, 7)))
 
 
 def entries(list_tile, first, last):
@@ -55,54 +55,46 @@ def tile_picked_hub_silu_p_kernel(
         src_t = lists.tile([P, U // LIST_ROWS], U16, name="src_t")
         dst_t = lists.tile([P, U // LIST_ROWS], U16, name="dst_t")
 
-        xs_all = keep.tile([P, T], U8, name="xs_all", align_bytes=64)
-        w3_s = keep.tile([P, N], U8, name="w3_s", align_bytes=64)
-        w3_c = keep.tile([P, N], U32, name="w3_c", align_bytes=64)
-        nc.vector.memset(xs_all[:].bitcast(I32), 0)
-        nc.gpsimd.memset(w3_s[:].bitcast(I32), 0)
+        xs_all = keep.tile([P, T], U8, name="xs_all", tag="xs_all", align_bytes=64)
+        xs = keep.tile([P, S], U8, name="xs", align_bytes=64)
+        nc.vector.memset(xs_all[QUADRANT : 2 * QUADRANT].bitcast(I32), 0)
+        nc.vector.memset(xs_all[2 * QUADRANT :].bitcast(I32), 0)
+        nc.gpsimd.memset(xs[:].bitcast(I32), 0)
 
-        xw_all = [keep.tile([P, T], U32, name=f"xw_all{g}", tag=f"xw_all{g}", align_bytes=64) for g in range(PASSES)]
-        raw = {
-            (a, g): keep.tile([P, PACK, H], F32, name=f"raw{a}{g}", align_bytes=64)
-            for a in (Y, E)
-            for g in range(PASSES)
-            if (a, g) != (Y, 1)
-        }
+        xw_all = {}
+        raw = {}
 
-        def load_words(g):
+        def load_words(g, tag):
+            xw_all[g] = keep.tile([P, T], U32, name=f"xw_all{g}", tag=tag, align_bytes=64)
             nc.sync.dma_start(
                 out=xw_all[g][:].bitcast(I32), in_=x_words[g].rearrange("p n t -> p (n t)").bitcast(I32)
             )
 
-        def load_weight(a, g):
+        def load_weight(a, g, tag):
+            raw[a, g] = keep.tile([P, PACK, H], F32, name=f"raw{a}{g}", tag=tag, align_bytes=64)
             k_rows = (w1, w2)[a][g * K_PASS : (g + 1) * K_PASS, :]
             nc.sync.dma_start(out=raw[a, g][:], in_=k_rows.rearrange("(p j) c -> p j c", j=PACK))
 
-        load_words(0)
         nc.sync.dma_start(offs_t[:], offs)
-        for q in range(P // QUADRANT):
-            nc.sync.dma_start(
-                out=xs_all[QUADRANT * q : QUADRANT * q + PASSES * SCALE_ROWS, :].bitcast(I32),
-                in_=x_scales[:, SCALE_ROWS * q : SCALE_ROWS * (q + 1), :].bitcast(I32),
-            )
-        load_weight(Y, 0)
-        load_words(1)
-        late_rows = w1[K_PASS:, :].rearrange("(p j) c -> p j c", j=PACK)
-        late = [keep.tile([P, PACK, PACK * (m1 - m0)], F32, name=f"late{m0}", align_bytes=64) for m0, m1 in LATE_PIECES]
-        for tile, (m0, m1) in zip(late, LATE_PIECES):
-            nc.sync.dma_start(out=tile[:], in_=late_rows[:, :, PACK * m0 : PACK * m1])
-        nc.sync.dma_start(src_t[:], src)
         for g in range(PASSES):
-            load_weight(E, g)
-        nc.sync.dma_start(dst_t[:], dst)
-        nc.sync.dma_start(out=w3_c[:].bitcast(I32), in_=w3_words[0].rearrange("p n t -> p (n t)").bitcast(I32))
-        for q in range(P // QUADRANT):
             nc.sync.dma_start(
-                out=w3_s[QUADRANT * q : QUADRANT * q + SCALE_ROWS, :].bitcast(I32),
-                in_=w3_scales[0, SCALE_ROWS * q : SCALE_ROWS * (q + 1), :].bitcast(I32),
+                out=xs_all[16 * g : 16 * (g + 1), :].bitcast(I32),
+                in_=x_scales[g].rearrange("(q r) n -> r q n", r=SCALE_ROWS).bitcast(I32),
             )
+        load_words(0, "xw_all0")
+        load_weight(Y, 0, "raw00")
+        load_words(1, "xw_all1")
+        nc.sync.dma_start(src_t[:], src)
+        nc.sync.dma_start(dst_t[:], dst)
+        late_rows = w1[K_PASS:, :].rearrange("(p j) c -> p j c", j=PACK)
+        late = []
 
-        xs = keep.tile([P, S], U8, name="xs", align_bytes=64)
+        def load_late(tag):
+            m0, m1 = LATE_PIECES[len(late)]
+            late.append(keep.tile([P, PACK, PACK * (m1 - m0)], F32, name=f"late{m0}", tag=tag, align_bytes=64))
+            nc.sync.dma_start(out=late[-1][:], in_=late_rows[:, :, PACK * m0 : PACK * m1])
+
+        picked = keep.tile([P, S], U8, name="picked", tag="picked", align_bytes=64)
         xw = {}
         codes, scales = {}, {}
 
@@ -122,9 +114,9 @@ def tile_picked_hub_silu_p_kernel(
             count = woven.shape[1]
             name = f"codes{a}{g}{first}"
             words = keep.tile([P, count * P], U32, name=name, tag=tag or name, align_bytes=64)
-            plane = keep.tile([P, count * P], U8, name=f"scales{a}{g}{first}", align_bytes=64)
+            plane = keep.tile([P, count * P], U8, name=f"scales{a}{g}{first}", tag=f"scales{a}{g}{first}", align_bytes=64)
             nc.vector.quantize_mx(
-                out=words[:].bitcast(FP8X4), scales=plane[:], in_=woven[:].rearrange("p t m j -> p (t m j)")
+                out=words[:].bitcast(FP8X4), scales=plane[:], in_=woven[:, :].rearrange("p t m j -> p (t m j)")
             )
             for n in range(count):
                 codes[a, g, first + n] = words[:, n * P : (n + 1) * P]
@@ -135,19 +127,16 @@ def tile_picked_hub_silu_p_kernel(
             weave(a, g, first, copy, woven[:])
             return woven
 
-        def woven_late(first, copies):
-            woven = woven_tile(Y, 1, first, PAIR)
-            laid = woven[:].rearrange("p t m j -> p m j t")
-            for tile, (m0, m1), copy in zip(late, LATE_PIECES, copies):
-                dealt = tile[:].rearrange("p j (m t) -> p m j t", t=PACK)[:, :, :, first : first + PAIR]
-                copy(out=laid[:, m0:m1], in_=dealt)
-            return woven
+        def weave_late(first, woven, piece, m0, m1, copy):
+            dealt = late[piece][:].rearrange("p j (m t) -> p m j t", t=PACK)[:, :, :, first : first + PAIR]
+            base = LATE_PIECES[piece][0]
+            copy(out=woven[:].rearrange("p t m j -> p m j t")[:, m0:m1], in_=dealt[:, m0 - base : m1 - base])
 
         banks = {}
 
         def product_pass(a, g, t, h):
             if g == 0:
-                banks[a, t, h] = psum.tile([P, BANK], F32, name=f"bank{a}{t}{h}", tag=f"bank{BANK_PAIRS[a][t]}{h}")
+                banks[a, t, h] = psum.tile([P, BANK], F32, name=f"bank{a}{t}{h}", tag=f"bank{TILE_BANKS[a][t][h]}")
             picked = slice(h * BANK, (h + 1) * BANK)
             nc.tensor.matmul_mx(
                 out=banks[a, t, h][:],
@@ -159,7 +148,7 @@ def tile_picked_hub_silu_p_kernel(
                 stop=(g == PASSES - 1),
             )
 
-        quarters = [psum.tile([P, BANK // 2], F32, name=f"quarter{n}", tag=f"bank{(0, 3)[n // 2]}{n % 2}") for n in range(4)]
+        quarters = [psum.tile([P, BANK // 2], F32, name=f"quarter{n}", tag=f"bank{(0, 1, 6, 7)[n]}") for n in range(4)]
 
         def first_tile_pass(g):
             for n in range(4):
@@ -201,41 +190,56 @@ def tile_picked_hub_silu_p_kernel(
             window = y_all[:, y_start[t] : y_start[t] + Y_WINDOW]
             nc.vector.tensor_copy(out=fetched[t][:], in_=window.indirect(src_t[:]))
 
+        nc.vector.tensor_copy(out=picked[:], in_=xs_all[:].indirect(offs_t[:]))
+        for q in range(P // QUADRANT):
+            nc.sync.dma_start(
+                out=xs[QUADRANT * q : QUADRANT * q + PASSES * SCALE_ROWS, :].bitcast(I32),
+                in_=picked[q:QUADRANT:SCALE_ROWS, :].bitcast(I32),
+            )
         gather_words(0, "xw0")
-        nc.vector.tensor_copy(out=xs[:], in_=xs_all[:].indirect(offs_t[:]))
-        quantise(Y, 0, 0, woven_pair(Y, 0, 0, on_scalar))
-        late_pass0 = woven_pair(Y, 0, PAIR, on_scalar)
+        load_late("xs_all")
+        load_late("xw_all0")
+        early = woven_pair(Y, 0, 0, on_scalar)
+        quantise(Y, 0, PAIR, woven_pair(Y, 0, PAIR, on_vector))
+        quantise(Y, 0, 0, early)
+        load_weight(E, 0, "raw00")
         gather_words(1, "xw1")
+        load_weight(E, 1, "xw_all1")
         first_tile_pass(0)
         for h in range(HALVES):
             product_pass(Y, 0, 1, h)
-        quantise(Y, 1, 0, woven_late(0, (on_scalar, on_scalar)))
+        lower, upper = woven_tile(Y, 1, 0, PAIR), woven_tile(Y, 1, PAIR, PAIR)
+        cut = LATE_PIECES[0][1]
+        weave_late(0, lower, 0, 0, cut, on_scalar)
+        weave_late(0, lower, 1, cut, P, on_vector)
+        quantise(Y, 1, 0, lower[:, :1])
         first_tile_pass(1)
+        quantise(Y, 1, 1, lower[:, 1:])
         for h in range(HALVES):
             product_pass(Y, 1, 1, h)
-        quantise(Y, 0, PAIR, late_pass0, "woven010")
-        late_pass1 = woven_late(PAIR, (on_scalar, on_vector))
-
+        weave_late(PAIR, upper, 0, 0, P // 2, on_scalar)
+        weave_late(PAIR, upper, 1, cut, P, on_vector)
+        weave_late(PAIR, upper, 0, P // 2, cut, on_vector)
         for n in range(4):
-            copy = (on_scalar, on_vector)[n % 2]
+            copy = on_vector if n == 1 else on_scalar
             copy(out=results[Y, 0][:, n * BANK // 2 : (n + 1) * BANK // 2], in_=quarters[n][:])
-        quantise(Y, 1, PAIR, late_pass1, "woven002")
-        for h in range(HALVES):
-            for g in range(PASSES):
-                product_pass(Y, g, PAIR, h)
+        w3_c = keep.tile([P, N], U32, name="w3_c", tag="xs_all", align_bytes=64)
+        nc.sync.dma_start(out=w3_c[:].bitcast(I32), in_=w3_words[0].rearrange("p n t -> p (n t)").bitcast(I32))
+        quantise(Y, 1, PAIR, upper)
         fetch_sources(0)
-        for h in range(HALVES):
-            for g in range(PASSES):
-                product_pass(Y, g, PACK - 1, h)
+        for t in range(PAIR, PACK):
+            for h in range(HALVES):
+                for g in range(PASSES):
+                    product_pass(Y, g, t, h)
         empty_tile(Y, 1)
         fetch_sources(1)
-        quantise(E, 0, 0, woven_pair(E, 0, 0, on_scalar, "codes010"))
+        quantise(E, 0, 0, woven_pair(E, 0, 0, on_scalar, "codes011"))
         empty_tile(Y, 2)
         fetch_sources(2)
-        quantise(E, 1, 0, woven_pair(E, 1, 0, on_scalar, "scales010"))
+        quantise(E, 1, 0, woven_pair(E, 1, 0, on_scalar, "scales012"))
         empty_tile(Y, 3)
         fetch_sources(3)
-        woven = woven_tile(E, 0, PAIR, PASSES * PAIR, "woven002")
+        woven = woven_tile(E, 0, PAIR, PASSES * PAIR, "codes012")
         for g in range(PASSES):
             weave(E, g, PAIR, on_scalar, woven[:, PAIR * g : PAIR * (g + 1)])
         quantise(E, 0, PAIR, woven)
@@ -247,10 +251,18 @@ def tile_picked_hub_silu_p_kernel(
                     product_pass(E, g, t, h)
             empty_tile(E, t)
 
+        w3_s = keep.tile([P, N], U8, name="w3_s", tag="scales110", align_bytes=64)
+        nc.gpsimd.memset(w3_s[:].bitcast(I32), 0)
+        for q in range(P // QUADRANT):
+            nc.sync.dma_start(
+                out=w3_s[QUADRANT * q : QUADRANT * q + SCALE_ROWS, :].bitcast(I32),
+                in_=w3_scales[0, SCALE_ROWS * q : SCALE_ROWS * (q + 1), :].bitcast(I32),
+            )
+
         out_v = out.rearrange("(mt p) r -> p mt r", p=P)
         ring = ctx.enter_context(tc.tile_pool(name="ring", bufs=2))
 
-        def finish(first, widths, z, copy=on_scalar):
+        def finish(first, widths, z, copies=(on_scalar,)):
             start = first
             for width in widths:
                 last = first + width
@@ -259,13 +271,15 @@ def tile_picked_hub_silu_p_kernel(
                 values = z[:, (first - start) * PACK : (last - start) * PACK]
                 nc.vector.quantize_mx(out=z_words[:].bitcast(FP8X4), scales=z_scales[:], in_=values)
                 res = keep.tile([P, N // P, width], F32, name=f"res{first}", align_bytes=64)
-                bank = "bank%d%d" % divmod((len(done) + 6) % PSUM_BANKS, HALVES)
-                done.append(first)
-                acc = psum.tile([P, N // P, width], F32, name=f"acc{first}", tag=bank)
+                shared = len(copies) > 1
+                acc = [
+                    psum.tile([P, N // P // len(copies), width], F32, name=f"acc{first}{n}", tag=f"bank{out_banks.pop(0)}")
+                    for n in range(len(copies))
+                ]
                 for block in range(N // P):
                     cols = slice(block * P, (block + 1) * P)
                     nc.tensor.matmul_mx(
-                        out=acc[:, block, :],
+                        out=acc[block][:, 0, :] if shared else acc[0][:, block, :],
                         lhsT=w3_c[:, cols].bitcast(FP8X4),
                         lhsT_scale=w3_s[:, cols],
                         rhs=z_words[:].bitcast(FP8X4),
@@ -273,7 +287,8 @@ def tile_picked_hub_silu_p_kernel(
                         start=True,
                         stop=True,
                     )
-                copy(out=res[:], in_=acc[:])
+                for n, copy in enumerate(copies):
+                    copy(out=res[:, n : n + 1] if shared else res[:], in_=acc[n][:])
                 nc.sync.dma_start(out=out_v[:, :, first:last], in_=res[:])
                 first = last
 
@@ -285,7 +300,7 @@ def tile_picked_hub_silu_p_kernel(
                 op=ADD,
             )
 
-        done, waiting, first = [], None, 0
+        out_banks, waiting, first = [4, 5, 2, 3, 0, 1], None, 0
         for widths in EDGE_SLICES:
             last = first + sum(widths)
             u = ring.tile([P, PACK, last - first], F32, name=f"u{first}", tag="u", align_bytes=64)
@@ -305,4 +320,4 @@ def tile_picked_hub_silu_p_kernel(
                 finish(*waiting)
             waiting = first, widths, z
             first = last
-        finish(*waiting, on_vector)
+        finish(*waiting, (on_vector, on_scalar))

@@ -260,7 +260,16 @@ def tile_picked_hub_silu_p_kernel(
             )
 
         out_v = out.rearrange("(mt p) r -> p mt r", p=P)
-        ring = ctx.enter_context(tc.tile_pool(name="ring", bufs=2))
+        wide, narrow = PACK * sum(EDGE_SLICES[1]), PACK * sum(EDGE_SLICES[2])
+        sums = keep.tile([P, wide + narrow], F32, name="sums", align_bytes=64)
+        end = sum(EDGE_SLICES[3])
+        third = sums[:, wide:].rearrange("p (t r) -> p t r", t=PACK)
+        places = [
+            third[:, :, : sum(EDGE_SLICES[0])],
+            sums[:, :wide].rearrange("p (t r) -> p t r", t=PACK),
+            third,
+            sums[:, wide - (PACK - 1) * end : wide + end].rearrange("p (t r) -> p t r", t=PACK),
+        ]
 
         def finish(first, widths, z, copies=(on_scalar,)):
             start = first
@@ -300,12 +309,14 @@ def tile_picked_hub_silu_p_kernel(
                 op=ADD,
             )
 
-        out_banks, waiting, first = [4, 5, 2, 3, 0, 1], None, 0
-        for widths in EDGE_SLICES:
+        out_banks, waiting, first = [4, 5, 2, 3, 0, 1, 6], None, 0
+        for u, widths in zip(places, EDGE_SLICES):
             last = first + sum(widths)
-            u = ring.tile([P, PACK, last - first], F32, name=f"u{first}", tag="u", align_bytes=64)
             for t in range(PACK - 1):
                 join(u, t, first, first, last)
+            if last == U:
+                finish(*waiting, (on_vector, on_scalar))
+                waiting = None
             z = keep.tile([P, (last - first) * PACK], BF16, name=f"z{first}", align_bytes=64)
             at = 0
             for width in widths:

@@ -271,6 +271,8 @@ def tile_picked_hub_silu_p_kernel(
             sums[:, wide - (PACK - 1) * end : wide + end].rearrange("p (t r) -> p t r", t=PACK),
         ]
 
+        filled = []
+
         def finish(first, widths, z, copies=(on_scalar,)):
             start = first
             for width in widths:
@@ -278,28 +280,40 @@ def tile_picked_hub_silu_p_kernel(
                 z_words = keep.tile([P, width], U32, name=f"zc{first}", align_bytes=64)
                 z_scales = keep.tile([P, width], U8, name=f"zs{first}", align_bytes=64)
                 values = z[:, (first - start) * PACK : (last - start) * PACK]
-                nc.vector.quantize_mx(out=z_words[:].bitcast(FP8X4), scales=z_scales[:], in_=values)
                 res = keep.tile([P, N // P, width], F32, name=f"res{first}", align_bytes=64)
                 shared = len(copies) > 1
                 acc = [
                     psum.tile([P, N // P // len(copies), width], F32, name=f"acc{first}{n}", tag=f"bank{out_banks.pop(0)}")
                     for n in range(len(copies))
                 ]
-                for block in range(N // P):
-                    cols = slice(block * P, (block + 1) * P)
-                    nc.tensor.matmul_mx(
-                        out=acc[block][:, 0, :] if shared else acc[0][:, block, :],
-                        lhsT=w3_c[:, cols].bitcast(FP8X4),
-                        lhsT_scale=w3_s[:, cols],
-                        rhs=z_words[:].bitcast(FP8X4),
-                        rhs_scale=z_scales[:],
-                        start=True,
-                        stop=True,
+                step = width // 2 if last == U else width
+                for at in range(0, width, step):
+                    part = slice(at, at + step)
+                    nc.vector.quantize_mx(
+                        out=z_words[:, part].bitcast(FP8X4),
+                        scales=z_scales[:, part],
+                        in_=values[:, at * PACK : (at + step) * PACK],
                     )
-                for n, copy in enumerate(copies):
-                    copy(out=res[:, n : n + 1] if shared else res[:], in_=acc[n][:])
-                nc.sync.dma_start(out=out_v[:, :, first:last], in_=res[:])
+                    for block in range(N // P):
+                        cols = slice(block * P, (block + 1) * P)
+                        nc.tensor.matmul_mx(
+                            out=acc[block][:, 0, part] if shared else acc[0][:, block, part],
+                            lhsT=w3_c[:, cols].bitcast(FP8X4),
+                            lhsT_scale=w3_s[:, cols],
+                            rhs=z_words[:, part].bitcast(FP8X4),
+                            rhs_scale=z_scales[:, part],
+                            start=True,
+                            stop=True,
+                        )
+                filled.append((first, last, res, acc, copies))
                 first = last
+
+        def store():
+            while filled:
+                first, last, res, acc, copies = filled.pop(0)
+                for n, copy in enumerate(copies):
+                    copy(out=res[:, n : n + 1] if len(copies) > 1 else res[:], in_=acc[n][:])
+                nc.sync.dma_start(out=out_v[:, :, first:last], in_=res[:])
 
         def join(u, t, start, first, last):
             nc.vector.tensor_tensor(
@@ -319,7 +333,7 @@ def tile_picked_hub_silu_p_kernel(
                 waiting = None
             z = keep.tile([P, (last - first) * PACK], BF16, name=f"z{first}", align_bytes=64)
             at = 0
-            for width in widths:
+            for width in widths if last < U else (widths[0] // 2,) * 2:
                 join(u, PACK - 1, first, first + at, first + at + width)
                 nc.scalar.activation(
                     out=z[:, at * PACK : (at + width) * PACK].rearrange("p (c i t) -> p c t i", i=PACK, t=PACK),
@@ -329,6 +343,8 @@ def tile_picked_hub_silu_p_kernel(
                 at += width
             if waiting:
                 finish(*waiting)
+            store()
             waiting = first, widths, z
             first = last
         finish(*waiting, (on_vector, on_scalar))
+        store()

@@ -312,8 +312,12 @@ def tile_picked_hub_silu_p_kernel(
             while filled:
                 first, last, res, acc, copies = filled.pop(0)
                 for n, copy in enumerate(copies):
-                    copy(out=res[:, n : n + 1] if len(copies) > 1 else res[:], in_=acc[n][:])
-                nc.sync.dma_start(out=out_v[:, :, first:last], in_=res[:])
+                    part = slice(n, n + 1) if len(copies) > 1 else slice(0, N // P)
+                    copy(out=res[:, part], in_=acc[n][:])
+                    if last < U:
+                        nc.sync.dma_start(out=out_v[:, part, first:last], in_=res[:, part])
+                if last == U:
+                    nc.sync.dma_start(out=out_v[:, :, first:last], in_=res[:])
 
         def join(u, t, start, first, last):
             nc.vector.tensor_tensor(

@@ -14,6 +14,7 @@ U8 = mybir.dt.uint8
 FP8X4 = mybir.dt.float8_e4m3fn_x4
 ADD = mybir.AluOpType.add
 SILU = mybir.ActivationFunctionType.Silu
+COPY = mybir.ActivationFunctionType.Copy
 
 P = 128
 PACK = 4
@@ -28,8 +29,7 @@ QUADRANT = 32
 SCALE_ROWS = 4
 Y, E = 0, 1
 
-Y_WINDOW = 1376
-E_WINDOW = S + LIST_ROWS
+Y_WINDOW = S + LIST_ROWS
 
 EDGE_SLICES = ((128,),(256,256,),(256,),(128,),)
 
@@ -110,6 +110,11 @@ def tile_picked_hub_silu_p_kernel(
             dealt = raw[a, g][:].rearrange("p j (m t) -> p m j t", t=PACK)[:, :, :, first : first + PAIR]
             copy(out=woven.rearrange("p t m j -> p m j t"), in_=dealt)
 
+        def woven_whole(a, g, copy):
+            woven = woven_tile(a, g, 0, PACK)
+            copy(out=woven[:].rearrange("p t m j -> p m j t"), in_=raw[a, g][:].rearrange("p j (m t) -> p m j t", t=PACK))
+            return woven
+
         def quantise(a, g, first, woven, tag=None):
             count = woven.shape[1]
             name = f"codes{a}{g}{first}"
@@ -168,27 +173,30 @@ def tile_picked_hub_silu_p_kernel(
                 for h in range(HALVES):
                     product_pass(a, g, t, h)
 
-        y_all = keep.tile([P, (PACK - 1) * S + Y_WINDOW], F32, name="y_all", align_bytes=64)
-        nc.gpsimd.memset(y_all[:, PACK * S :], 0.0)
+        y_all = [keep.tile([P, Y_WINDOW], F32, name=f"y_all{t}", align_bytes=64) for t in range(PACK)]
+        for t in range(PACK):
+            nc.gpsimd.memset(y_all[t][:, S:], 0.0)
         warm = keep.tile([P, 1], F32, name="warm")
-        nc.scalar.activation(out=warm[:], in_=y_all[:, PACK * S : PACK * S + 1], func=SILU)
+        nc.scalar.activation(out=warm[:], in_=y_all[0][:, S : S + 1], func=SILU)
         e_all = [keep.tile([P, S], F32, name=f"e_all{t}", align_bytes=64) for t in range(PACK)]
-        y_start = [(PACK - 1 - t) * S for t in range(PACK)]
-        results = {(Y, t): y_all[:, y_start[t] : y_start[t] + S] for t in range(PACK)}
+        results = {(Y, t): y_all[t][:, :S] for t in range(PACK)}
         results.update({(E, t): e_all[t][:, :S] for t in range(PACK)})
 
         def empty_bank(a, t, h, copy=on_scalar):
             copy(out=results[a, t][:, h * BANK : (h + 1) * BANK], in_=banks[a, t, h][:])
 
-        def empty_tile(a, t):
+        def empty_tile(a, t, copy=on_scalar):
             for h in range(HALVES):
-                empty_bank(a, t, h)
+                empty_bank(a, t, h, copy)
 
-        fetched = [keep.tile([P, U], F32, name=f"fetched{t}", align_bytes=64) for t in range(PACK)]
+        fetched = {}
 
-        def fetch_sources(t):
-            window = y_all[:, y_start[t] : y_start[t] + Y_WINDOW]
-            nc.vector.tensor_copy(out=fetched[t][:], in_=window.indirect(src_t[:]))
+        def fetch_sources(t, first=0, last=U, tag=None):
+            if first == 0:
+                fetched[t] = keep.tile([P, U], F32, name=f"fetched{t}", tag=tag or f"fetched{t}", align_bytes=64)
+            nc.scalar.activation(
+                out=fetched[t][:, first:last], in_=y_all[t][:].indirect(entries(src_t, first, last)), func=COPY
+            )
 
         nc.vector.tensor_copy(out=picked[:], in_=xs_all[:].indirect(offs_t[:]))
         for q in range(P // QUADRANT):
@@ -231,27 +239,26 @@ def tile_picked_hub_silu_p_kernel(
             for h in range(HALVES):
                 for g in range(PASSES):
                     product_pass(Y, g, t, h)
-        empty_tile(Y, 1)
-        fetch_sources(1)
-        quantise(E, 0, 0, woven_pair(E, 0, 0, on_scalar, "codes011"))
-        empty_tile(Y, 2)
-        fetch_sources(2)
-        quantise(E, 1, 0, woven_pair(E, 1, 0, on_scalar, "scales012"))
+        empty_tile(Y, 1, on_vector)
+        woven = woven_whole(E, 0, on_vector)
+        empty_tile(Y, 2, on_vector)
         empty_tile(Y, 3)
-        fetch_sources(3)
-        woven = woven_tile(E, 0, PAIR, PASSES * PAIR, "codes012")
-        for g in range(PASSES):
-            weave(E, g, PAIR, on_scalar, woven[:, PAIR * g : PAIR * (g + 1)])
-        quantise(E, 0, PAIR, woven)
-        for n in range(PAIR):
-            codes[E, 1, PAIR + n], scales[E, 1, PAIR + n] = codes[E, 0, PACK + n], scales[E, 0, PACK + n]
+        fetch_sources(1)
+        quantise(E, 0, 0, woven)
         for t in range(PACK):
             for h in range(HALVES):
-                for g in range(PASSES):
-                    product_pass(E, g, t, h)
-            empty_tile(E, t)
+                product_pass(E, 0, t, h)
+        woven = woven_whole(E, 1, on_vector)
+        fetch_sources(2)
+        quantise(E, 1, 0, woven)
+        for t in range(PACK):
+            for h in range(HALVES):
+                product_pass(E, 1, t, h)
+            empty_tile(E, t, on_vector if t == 0 else on_scalar)
+        for first, last in ((0, 384), (384, 640), (640, U)):
+            fetch_sources(PACK - 1, first, last, "codes110")
 
-        w3_s = keep.tile([P, N], U8, name="w3_s", tag="scales110", align_bytes=64)
+        w3_s = keep.tile([P, N], U8, name="w3_s", tag="scales100", align_bytes=64)
         nc.gpsimd.memset(w3_s[:].bitcast(I32), 0)
         for q in range(P // QUADRANT):
             nc.sync.dma_start(

@@ -229,7 +229,7 @@ def tile_picked_hub_silu_p_kernel(
         weave_late(PAIR, upper, 1, cut, P, on_vector)
         weave_late(PAIR, upper, 0, P // 2, cut, on_vector)
         for n in range(4):
-            copy = on_vector if n == 1 else on_scalar
+            copy = on_vector if n % 2 else on_scalar
             copy(out=results[Y, 0][:, n * BANK // 2 : (n + 1) * BANK // 2], in_=quarters[n][:])
         w3_c = keep.tile([P, N], U32, name="w3_c", tag="xs_all", align_bytes=64)
         nc.sync.dma_start(out=w3_c[:].bitcast(I32), in_=w3_words[0].rearrange("p n t -> p (n t)").bitcast(I32))
@@ -241,22 +241,27 @@ def tile_picked_hub_silu_p_kernel(
                     product_pass(Y, g, t, h)
         empty_tile(Y, 1, on_vector)
         woven = woven_whole(E, 0, on_vector)
-        empty_tile(Y, 2, on_vector)
-        empty_tile(Y, 3)
         fetch_sources(1)
+        empty_tile(Y, 2, on_vector)
         quantise(E, 0, 0, woven)
-        for t in range(PACK):
-            for h in range(HALVES):
-                product_pass(E, 0, t, h)
-        woven = woven_whole(E, 1, on_vector)
+        product_pair(E, 0, 0)
         fetch_sources(2)
+        woven = woven_pair(E, 1, 0, on_vector)
+        empty_bank(Y, 3, 0, on_vector)
         quantise(E, 1, 0, woven)
-        for t in range(PACK):
+        product_pair(E, 1, 0)
+        woven = woven_pair(E, 1, PAIR, on_vector)
+        empty_bank(Y, 3, 1, on_vector)
+        quantise(E, 1, PAIR, woven)
+        empty_tile(E, 0, on_vector)
+        empty_tile(E, 1)
+        for t in range(PAIR, PACK):
             for h in range(HALVES):
-                product_pass(E, 1, t, h)
-            empty_tile(E, t, on_vector if t == 0 else on_scalar)
+                for g in range(PASSES):
+                    product_pass(E, g, t, h)
+            empty_tile(E, t)
         for first, last in ((0, 384), (384, 640), (640, U)):
-            fetch_sources(PACK - 1, first, last, "codes110")
+            fetch_sources(PACK - 1, first, last, "codes112")
 
         w3_s = keep.tile([P, N], U8, name="w3_s", tag="scales100", align_bytes=64)
         nc.gpsimd.memset(w3_s[:].bitcast(I32), 0)

@@ -34,7 +34,7 @@ Y_WINDOW = S + LIST_ROWS
 EDGE_SLICES = ((128,),(256,256,),(256,),(128,),)
 
 LATE_PIECES = ((0, 96), (96, 128))
-TILE_BANKS = ((None, (2, 3), (0, 1), (6, 7)), ((4, 5), (2, 3), (0, 1), (6, 7)))
+TILE_BANKS = ((None, (2, 3), (0, 1), (3, 0)), ((4, 5), (6, 7), (2, 1), (3, 0)))
 
 
 def entries(list_tile, first, last):
@@ -56,10 +56,11 @@ def tile_picked_hub_silu_p_kernel(
         dst_t = lists.tile([P, U // LIST_ROWS], U16, name="dst_t")
 
         xs_all = keep.tile([P, T], U8, name="xs_all", tag="xs_all", align_bytes=64)
-        xs = keep.tile([P, S], U8, name="xs", align_bytes=64)
+        xs = [keep.tile([P, S], U8, name=f"xs{g}", align_bytes=64) for g in range(PASSES)]
         nc.vector.memset(xs_all[QUADRANT : 2 * QUADRANT].bitcast(I32), 0)
         nc.vector.memset(xs_all[2 * QUADRANT :].bitcast(I32), 0)
-        nc.gpsimd.memset(xs[:].bitcast(I32), 0)
+        for g in range(PASSES):
+            nc.gpsimd.memset(xs[g][:].bitcast(I32), 0)
 
         xw_all = {}
         raw = {}
@@ -76,11 +77,7 @@ def tile_picked_hub_silu_p_kernel(
             nc.sync.dma_start(out=raw[a, g][:], in_=k_rows.rearrange("(p j) c -> p j c", j=PACK))
 
         nc.sync.dma_start(offs_t[:], offs)
-        for g in range(PASSES):
-            nc.sync.dma_start(
-                out=xs_all[16 * g : 16 * (g + 1), :].bitcast(I32),
-                in_=x_scales[g].rearrange("(q r) n -> r q n", r=SCALE_ROWS).bitcast(I32),
-            )
+        nc.sync.dma_start(out=xs_all[:QUADRANT, :].bitcast(I32), in_=x_scales.rearrange("g r n -> (g r) n").bitcast(I32))
         load_words(0, "xw_all0")
         load_weight(Y, 0, "raw00")
         load_words(1, "xw_all1")
@@ -148,7 +145,7 @@ def tile_picked_hub_silu_p_kernel(
                 lhsT=codes[a, g, t].bitcast(FP8X4),
                 lhsT_scale=scales[a, g, t],
                 rhs=xw[g][:, picked].bitcast(FP8X4),
-                rhs_scale=xs[SCALE_ROWS * g :, picked],
+                rhs_scale=xs[g][:, picked],
                 start=(g == 0),
                 stop=(g == PASSES - 1),
             )
@@ -163,7 +160,7 @@ def tile_picked_hub_silu_p_kernel(
                     lhsT=codes[Y, g, 0].bitcast(FP8X4),
                     lhsT_scale=scales[Y, g, 0],
                     rhs=xw[g][:, picked].bitcast(FP8X4),
-                    rhs_scale=xs[SCALE_ROWS * g :, picked],
+                    rhs_scale=xs[g][:, picked],
                     start=(g == 0),
                     stop=(g == PASSES - 1),
                 )
@@ -199,14 +196,20 @@ def tile_picked_hub_silu_p_kernel(
             )
 
         nc.vector.tensor_copy(out=picked[:], in_=xs_all[:].indirect(offs_t[:]))
-        for q in range(P // QUADRANT):
-            nc.sync.dma_start(
-                out=xs[QUADRANT * q : QUADRANT * q + PASSES * SCALE_ROWS, :].bitcast(I32),
-                in_=picked[q:QUADRANT:SCALE_ROWS, :].bitcast(I32),
-            )
+
+
+        def place_scale_rows(g):
+            for q in range(P // QUADRANT):
+                to, at = QUADRANT * q, SCALE_ROWS * (P // QUADRANT * g + q)
+                nc.sync.dma_start(
+                    out=xs[g][to : to + SCALE_ROWS, :].bitcast(I32), in_=picked[at : at + SCALE_ROWS, :].bitcast(I32)
+                )
+
+        place_scale_rows(0)
         gather_words(0, "xw0")
         load_late("xs_all")
         load_late("xw_all0")
+        place_scale_rows(1)
         early = woven_pair(Y, 0, 0, on_scalar)
         quantise(Y, 0, PAIR, woven_pair(Y, 0, PAIR, on_vector))
         quantise(Y, 0, 0, early)
@@ -245,14 +248,14 @@ def tile_picked_hub_silu_p_kernel(
         empty_tile(Y, 2, on_vector)
         quantise(E, 0, 0, woven)
         product_pair(E, 0, 0)
+        empty_bank(Y, 3, 0)
         fetch_sources(2)
         woven = woven_pair(E, 1, 0, on_vector)
-        empty_bank(Y, 3, 0, on_vector)
+        upper = woven_pair(E, 1, PAIR, on_vector)
         quantise(E, 1, 0, woven)
         product_pair(E, 1, 0)
-        woven = woven_pair(E, 1, PAIR, on_vector)
         empty_bank(Y, 3, 1, on_vector)
-        quantise(E, 1, PAIR, woven)
+        quantise(E, 1, PAIR, upper)
         empty_tile(E, 0, on_vector)
         empty_tile(E, 1)
         for t in range(PAIR, PACK):

@@ -34,7 +34,7 @@ Y_WINDOW = S + LIST_ROWS
 EDGE_SLICES = ((128,),(256,256,),(256,),(128,),)
 
 LATE_PIECES = ((0, 96), (96, 128))
-TILE_BANKS = ((None, (2, 3), (0, 1), (3, 0)), ((4, 5), (6, 7), (2, 1), (3, 0)))
+TILE_BANKS = ((None, (2, 3), (4, 0), (1, 6)), ((5, 7), (2, 3), (4, 0), (1, 6)))
 
 
 def entries(list_tile, first, last):
@@ -106,11 +106,6 @@ def tile_picked_hub_silu_p_kernel(
         def weave(a, g, first, copy, woven):
             dealt = raw[a, g][:].rearrange("p j (m t) -> p m j t", t=PACK)[:, :, :, first : first + PAIR]
             copy(out=woven.rearrange("p t m j -> p m j t"), in_=dealt)
-
-        def woven_whole(a, g, copy):
-            woven = woven_tile(a, g, 0, PACK)
-            copy(out=woven[:].rearrange("p t m j -> p m j t"), in_=raw[a, g][:].rearrange("p j (m t) -> p m j t", t=PACK))
-            return woven
 
         def quantise(a, g, first, woven, tag=None):
             count = woven.shape[1]
@@ -217,8 +212,8 @@ def tile_picked_hub_silu_p_kernel(
         gather_words(1, "xw1")
         load_weight(E, 1, "xw_all1")
         first_tile_pass(0)
-        for h in range(HALVES):
-            product_pass(Y, 0, 1, h)
+        for t, h in ((1, 0), (1, 1), (2, 0)):
+            product_pass(Y, 0, t, h)
         lower, upper = woven_tile(Y, 1, 0, PAIR), woven_tile(Y, 1, PAIR, PAIR)
         cut = LATE_PIECES[0][1]
         weave_late(0, lower, 0, 0, cut, on_scalar)
@@ -238,24 +233,29 @@ def tile_picked_hub_silu_p_kernel(
         nc.sync.dma_start(out=w3_c[:].bitcast(I32), in_=w3_words[0].rearrange("p n t -> p (n t)").bitcast(I32))
         quantise(Y, 1, PAIR, upper)
         fetch_sources(0)
-        for t in range(PAIR, PACK):
-            for h in range(HALVES):
-                for g in range(PASSES):
-                    product_pass(Y, g, t, h)
+        product_pass(Y, 1, 2, 0)
+        for t, h in ((2, 1), (3, 0), (3, 1)):
+            for g in range(PASSES):
+                product_pass(Y, g, t, h)
         empty_tile(Y, 1, on_vector)
-        woven = woven_whole(E, 0, on_vector)
+        lower = woven_pair(E, 0, 0, on_vector)
         fetch_sources(1)
-        empty_tile(Y, 2, on_vector)
-        quantise(E, 0, 0, woven)
-        product_pair(E, 0, 0)
-        empty_bank(Y, 3, 0)
+        empty_bank(Y, 2, 0, on_vector)
+        empty_bank(Y, 2, 1)
         fetch_sources(2)
-        woven = woven_pair(E, 1, 0, on_vector)
-        upper = woven_pair(E, 1, PAIR, on_vector)
-        quantise(E, 1, 0, woven)
+        quantise(E, 0, 0, lower)
+        product_pair(E, 0, 0)
+        upper = woven_tile(E, 0, PAIR, PASSES * PAIR)
+        weave(E, 0, PAIR, on_vector, upper[:, :PAIR])
+        lower = woven_pair(E, 1, 0, on_vector)
+        empty_bank(Y, 3, 0, on_vector)
+        quantise(E, 1, 0, lower)
         product_pair(E, 1, 0)
+        weave(E, 1, PAIR, on_vector, upper[:, PAIR:])
         empty_bank(Y, 3, 1, on_vector)
-        quantise(E, 1, PAIR, upper)
+        quantise(E, 0, PAIR, upper)
+        for n in range(PAIR):
+            codes[E, 1, PAIR + n], scales[E, 1, PAIR + n] = codes[E, 0, PACK + n], scales[E, 0, PACK + n]
         empty_tile(E, 0, on_vector)
         empty_tile(E, 1)
         for t in range(PAIR, PACK):
@@ -264,7 +264,7 @@ def tile_picked_hub_silu_p_kernel(
                     product_pass(E, g, t, h)
             empty_tile(E, t)
         for first, last in ((0, 384), (384, 640), (640, U)):
-            fetch_sources(PACK - 1, first, last, "codes112")
+            fetch_sources(PACK - 1, first, last, "codes102")
 
         w3_s = keep.tile([P, N], U8, name="w3_s", tag="scales100", align_bytes=64)
         nc.gpsimd.memset(w3_s[:].bitcast(I32), 0)

@@ -73,7 +73,7 @@ def tile_picked_hub_silu_p_kernel(
 
         def load_weight(a, g, tag):
             raw[a, g] = keep.tile([P, PACK, H], F32, name=f"raw{a}{g}", tag=tag, align_bytes=64)
-            k_rows = (w1, w2)[a][g * K_PASS : (g + 1) * K_PASS, :]
+            k_rows = (w2, w1)[a][g * K_PASS : (g + 1) * K_PASS, :]
             nc.sync.dma_start(out=raw[a, g][:], in_=k_rows.rearrange("(p j) c -> p j c", j=PACK))
 
         nc.sync.dma_start(offs_t[:], offs)
@@ -83,7 +83,7 @@ def tile_picked_hub_silu_p_kernel(
         load_words(1, "xw_all1")
         nc.sync.dma_start(src_t[:], src)
         nc.sync.dma_start(dst_t[:], dst)
-        late_rows = w1[K_PASS:, :].rearrange("(p j) c -> p j c", j=PACK)
+        late_rows = w2[K_PASS:, :].rearrange("(p j) c -> p j c", j=PACK)
         late = []
 
         def load_late(tag):
@@ -187,7 +187,7 @@ def tile_picked_hub_silu_p_kernel(
             if first == 0:
                 fetched[t] = keep.tile([P, U], F32, name=f"fetched{t}", tag=tag or f"fetched{t}", align_bytes=64)
             nc.scalar.activation(
-                out=fetched[t][:, first:last], in_=y_all[t][:].indirect(entries(src_t, first, last)), func=COPY
+                out=fetched[t][:, first:last], in_=y_all[t][:].indirect(entries(dst_t, first, last)), func=COPY
             )
 
         nc.vector.tensor_copy(out=picked[:], in_=xs_all[:].indirect(offs_t[:]))
@@ -337,7 +337,7 @@ def tile_picked_hub_silu_p_kernel(
         def join(u, t, start, first, last):
             nc.vector.tensor_tensor(
                 out=u[:, t, first - start : last - start],
-                in0=e_all[t][:].indirect(entries(dst_t, first, last)),
+                in0=e_all[t][:].indirect(entries(src_t, first, last)),
                 in1=fetched[t][:, first:last],
                 op=ADD,
             )

@@ -17,24 +17,23 @@ SILU = mybir.ActivationFunctionType.Silu
 COPY = mybir.ActivationFunctionType.Copy
 
 P = 128
+HALF = P // 2
 PACK = 4
 PAIR = 2
 K_PASS = P * PACK
 PASSES = K // K_PASS
 BANK = 512
-PSUM_BANKS = 8
 HALVES = S // BANK
 LIST_ROWS = 16
 QUADRANT = 32
 SCALE_ROWS = 4
-Y, E = 0, 1
+E, Y = 0, 1
 
-Y_WINDOW = S + LIST_ROWS
+WINDOW = S + LIST_ROWS
 
-EDGE_SLICES = ((128,),(256,256,),(256,),(128,),)
-
+PIECES = (256, 256, 256, 128, 128)
 LATE_PIECES = ((0, 96), (96, 128))
-TILE_BANKS = ((None, (2, 3), (4, 0), (1, 6)), ((5, 7), (2, 3), (4, 0), (1, 6)))
+TILE_BANKS = ((None, (2, 3), (4, 0), (1, 6)), ((5, 7), (2, 3), (4, 0), (5, 7)))
 
 
 def entries(list_tile, first, last):
@@ -79,7 +78,7 @@ def tile_picked_hub_silu_p_kernel(
         nc.sync.dma_start(offs_t[:], offs)
         nc.sync.dma_start(out=xs_all[:QUADRANT, :].bitcast(I32), in_=x_scales.rearrange("g r n -> (g r) n").bitcast(I32))
         load_words(0, "xw_all0")
-        load_weight(Y, 0, "raw00")
+        load_weight(E, 0, "raw00")
         load_words(1, "xw_all1")
         nc.sync.dma_start(src_t[:], src)
         nc.sync.dma_start(dst_t[:], dst)
@@ -93,7 +92,7 @@ def tile_picked_hub_silu_p_kernel(
 
         picked = keep.tile([P, S], U8, name="picked", tag="picked", align_bytes=64)
         xw = {}
-        codes, scales = {}, {}
+        codes, scales, planes = {}, {}, {}
 
         def gather_words(g, tag):
             xw[g] = keep.tile([P, S], U32, name=f"xw{g}", tag=tag, align_bytes=64)
@@ -115,6 +114,7 @@ def tile_picked_hub_silu_p_kernel(
             nc.vector.quantize_mx(
                 out=words[:].bitcast(FP8X4), scales=plane[:], in_=woven[:, :].rearrange("p t m j -> p (t m j)")
             )
+            planes[a, g, first] = plane
             for n in range(count):
                 codes[a, g, first + n] = words[:, n * P : (n + 1) * P]
                 scales[a, g, first + n] = plane[:, n * P : (n + 1) * P]
@@ -152,8 +152,8 @@ def tile_picked_hub_silu_p_kernel(
                 picked = slice(n * BANK // 2, (n + 1) * BANK // 2)
                 nc.tensor.matmul_mx(
                     out=quarters[n][:],
-                    lhsT=codes[Y, g, 0].bitcast(FP8X4),
-                    lhsT_scale=scales[Y, g, 0],
+                    lhsT=codes[E, g, 0].bitcast(FP8X4),
+                    lhsT_scale=scales[E, g, 0],
                     rhs=xw[g][:, picked].bitcast(FP8X4),
                     rhs_scale=xs[g][:, picked],
                     start=(g == 0),
@@ -165,14 +165,14 @@ def tile_picked_hub_silu_p_kernel(
                 for h in range(HALVES):
                     product_pass(a, g, t, h)
 
-        y_all = [keep.tile([P, Y_WINDOW], F32, name=f"y_all{t}", align_bytes=64) for t in range(PACK)]
-        for t in range(PACK):
-            nc.gpsimd.memset(y_all[t][:, S:], 0.0)
+        e_all = [keep.tile([P, WINDOW], F32, name=f"e_all{t}", align_bytes=64) for t in range(PACK - 1)]
+        for t in range(PACK - 1):
+            nc.gpsimd.memset(e_all[t][:, S:], 0.0)
         warm = keep.tile([P, 1], F32, name="warm")
-        nc.scalar.activation(out=warm[:], in_=y_all[0][:, S : S + 1], func=SILU)
-        e_all = [keep.tile([P, S], F32, name=f"e_all{t}", align_bytes=64) for t in range(PACK)]
-        results = {(Y, t): y_all[t][:, :S] for t in range(PACK)}
-        results.update({(E, t): e_all[t][:, :S] for t in range(PACK)})
+        nc.scalar.activation(out=warm[:], in_=e_all[0][:, S : S + 1], func=SILU)
+        y_all = [keep.tile([P, S], F32, name=f"y_all{t}", align_bytes=64) for t in range(PACK)]
+        results = {(E, t): e_all[t][:, :S] for t in range(PACK - 1)}
+        results.update({(Y, t): y_all[t][:, :S] for t in range(PACK)})
 
         def empty_bank(a, t, h, copy=on_scalar):
             copy(out=results[a, t][:, h * BANK : (h + 1) * BANK], in_=banks[a, t, h][:])
@@ -187,7 +187,7 @@ def tile_picked_hub_silu_p_kernel(
             if first == 0:
                 fetched[t] = keep.tile([P, U], F32, name=f"fetched{t}", tag=tag or f"fetched{t}", align_bytes=64)
             nc.scalar.activation(
-                out=fetched[t][:, first:last], in_=y_all[t][:].indirect(entries(dst_t, first, last)), func=COPY
+                out=fetched[t][:, first:last], in_=e_all[t][:].indirect(entries(dst_t, first, last)), func=COPY
             )
 
         nc.vector.tensor_copy(out=picked[:], in_=xs_all[:].indirect(offs_t[:]))
@@ -205,69 +205,95 @@ def tile_picked_hub_silu_p_kernel(
         load_late("xs_all")
         load_late("xw_all0")
         place_scale_rows(1)
-        early = woven_pair(Y, 0, 0, on_scalar)
-        quantise(Y, 0, PAIR, woven_pair(Y, 0, PAIR, on_vector))
-        quantise(Y, 0, 0, early)
-        load_weight(E, 0, "raw00")
+        early = woven_pair(E, 0, 0, on_scalar)
+        quantise(E, 0, PAIR, woven_pair(E, 0, PAIR, on_vector))
+        quantise(E, 0, 0, early)
+        load_weight(Y, 0, "raw00")
         gather_words(1, "xw1")
-        load_weight(E, 1, "xw_all1")
+        load_weight(Y, 1, "xw_all1")
         first_tile_pass(0)
         for t, h in ((1, 0), (1, 1), (2, 0)):
-            product_pass(Y, 0, t, h)
-        lower, upper = woven_tile(Y, 1, 0, PAIR), woven_tile(Y, 1, PAIR, PAIR)
+            product_pass(E, 0, t, h)
+        lower, upper = woven_tile(E, 1, 0, PAIR), woven_tile(E, 1, PAIR, PAIR)
         cut = LATE_PIECES[0][1]
         weave_late(0, lower, 0, 0, cut, on_scalar)
         weave_late(0, lower, 1, cut, P, on_vector)
-        quantise(Y, 1, 0, lower[:, :1])
+        quantise(E, 1, 0, lower[:, :1])
         first_tile_pass(1)
-        quantise(Y, 1, 1, lower[:, 1:])
+        quantise(E, 1, 1, lower[:, 1:])
         for h in range(HALVES):
-            product_pass(Y, 1, 1, h)
+            product_pass(E, 1, 1, h)
         weave_late(PAIR, upper, 0, 0, P // 2, on_scalar)
         weave_late(PAIR, upper, 1, cut, P, on_vector)
         weave_late(PAIR, upper, 0, P // 2, cut, on_vector)
         for n in range(4):
             copy = on_vector if n % 2 else on_scalar
-            copy(out=results[Y, 0][:, n * BANK // 2 : (n + 1) * BANK // 2], in_=quarters[n][:])
+            copy(out=results[E, 0][:, n * BANK // 2 : (n + 1) * BANK // 2], in_=quarters[n][:])
         w3_c = keep.tile([P, N], U32, name="w3_c", tag="xs_all", align_bytes=64)
         nc.sync.dma_start(out=w3_c[:].bitcast(I32), in_=w3_words[0].rearrange("p n t -> p (n t)").bitcast(I32))
-        quantise(Y, 1, PAIR, upper)
+        quantise(E, 1, PAIR, upper)
         fetch_sources(0)
-        product_pass(Y, 1, 2, 0)
+        product_pass(E, 1, 2, 0)
         for t, h in ((2, 1), (3, 0), (3, 1)):
             for g in range(PASSES):
-                product_pass(Y, g, t, h)
-        empty_tile(Y, 1, on_vector)
-        lower = woven_pair(E, 0, 0, on_vector)
+                product_pass(E, g, t, h)
+        empty_tile(E, 1, on_vector)
+        lower = woven_pair(Y, 0, 0, on_vector)
         fetch_sources(1)
-        empty_bank(Y, 2, 0, on_vector)
-        empty_bank(Y, 2, 1)
+        empty_bank(E, 2, 0, on_vector)
+        empty_bank(E, 2, 1)
         fetch_sources(2)
-        quantise(E, 0, 0, lower)
-        product_pair(E, 0, 0)
-        upper = woven_tile(E, 0, PAIR, PASSES * PAIR)
-        weave(E, 0, PAIR, on_vector, upper[:, :PAIR])
-        lower = woven_pair(E, 1, 0, on_vector)
-        empty_bank(Y, 3, 0, on_vector)
-        quantise(E, 1, 0, lower)
-        product_pair(E, 1, 0)
-        weave(E, 1, PAIR, on_vector, upper[:, PAIR:])
-        empty_bank(Y, 3, 1, on_vector)
-        quantise(E, 0, PAIR, upper)
+        quantise(Y, 0, 0, lower)
+        product_pair(Y, 0, 0)
+        upper = woven_tile(Y, 0, PAIR, PASSES * PAIR)
+        weave(Y, 0, PAIR, on_vector, upper[:, :PAIR])
+        lower = woven_pair(Y, 1, 0, on_vector)
+        weave(Y, 1, PAIR, on_vector, upper[:, PAIR:])
+        quantise(Y, 1, 0, lower)
+        product_pair(Y, 1, 0)
+        quantise(Y, 0, PAIR, upper)
         for n in range(PAIR):
-            codes[E, 1, PAIR + n], scales[E, 1, PAIR + n] = codes[E, 0, PACK + n], scales[E, 0, PACK + n]
-        empty_tile(E, 0, on_vector)
-        empty_tile(E, 1)
+            codes[Y, 1, PAIR + n], scales[Y, 1, PAIR + n] = codes[Y, 0, PACK + n], scales[Y, 0, PACK + n]
+        empty_tile(Y, 0, on_vector)
+        empty_tile(Y, 1, on_vector)
         for t in range(PAIR, PACK):
             for h in range(HALVES):
                 for g in range(PASSES):
-                    product_pass(E, g, t, h)
-            empty_tile(E, t)
-        for first, last in ((0, 384), (384, 640), (640, U)):
-            fetch_sources(PACK - 1, first, last, "codes102")
+                    product_pass(Y, g, t, h)
+            empty_tile(Y, t)
+        sums = keep.tile([P, PACK * U - PIECES[0]], F32, name="sums", align_bytes=64)
+        early_sums, late_sums = sums[:, PACK * U // 2 - PIECES[0] :], sums[:, : PACK * U // 2]
+        u = [half.rearrange("p (t r) -> p t r", t=PACK) for half in (early_sums, late_sums)]
 
-        w3_s = keep.tile([P, N], U8, name="w3_s", tag="scales100", align_bytes=64)
-        nc.gpsimd.memset(w3_s[:].bitcast(I32), 0)
+        def sums_of(t, first, last):
+            h = first // (U // 2)
+            return u[h][:, t, first - h * U // 2 : last - h * U // 2]
+
+        def join(t, first, last):
+            h = first // (U // 2)
+            other = parked[h][:, first - h * U // 2 : last - h * U // 2] if t == PACK - 1 else fetched[t][:, first:last]
+            nc.vector.tensor_tensor(
+                out=sums_of(t, first, last),
+                in0=y_all[t][:].indirect(entries(src_t, first, last)),
+                in1=other,
+                op=ADD,
+            )
+
+        for t in range(PAIR):
+            join(t, 0, U // 2)
+            join(t, U // 2, U)
+        join(2, 0, U // 2)
+        e_all.append(keep.tile([P, S], F32, name="e_all3", tag="codes102", align_bytes=64))
+        results[E, 3] = e_all[3][:]
+        empty_tile(E, 3, on_scalar)
+        last_fetched = keep.tile([P, U // 2], F32, name="last_fetched", align_bytes=64)
+        parked = (sums_of(2, U // 2, U), last_fetched[:])
+        for h in range(2):
+            nc.scalar.activation(
+                out=parked[h], in_=e_all[3][:].indirect(entries(dst_t, h * U // 2, (h + 1) * U // 2)), func=COPY
+            )
+
+        w3_s = planes[Y, 1, 0]
         for q in range(P // QUADRANT):
             nc.sync.dma_start(
                 out=w3_s[QUADRANT * q : QUADRANT * q + SCALE_ROWS, :].bitcast(I32),
@@ -275,95 +301,81 @@ def tile_picked_hub_silu_p_kernel(
             )
 
         out_v = out.rearrange("(mt p) r -> p mt r", p=P)
-        wide, narrow = PACK * sum(EDGE_SLICES[1]), PACK * sum(EDGE_SLICES[2])
-        sums = keep.tile([P, wide + narrow], F32, name="sums", align_bytes=64)
-        end = sum(EDGE_SLICES[3])
-        third = sums[:, wide:].rearrange("p (t r) -> p t r", t=PACK)
-        places = [
-            third[:, :, : sum(EDGE_SLICES[0])],
-            sums[:, :wide].rearrange("p (t r) -> p t r", t=PACK),
-            third,
-            sums[:, wide - (PACK - 1) * end : wide + end].rearrange("p (t r) -> p t r", t=PACK),
-        ]
+        out_banks = [2, 3, 4, 0, 5, 7]
+        blocks = N // P
 
-        filled = []
-
-        def finish(first, widths, z, copies=(on_scalar,)):
-            start = first
-            for width in widths:
-                last = first + width
-                z_words = keep.tile([P, width], U32, name=f"zc{first}", align_bytes=64)
-                z_scales = keep.tile([P, width], U8, name=f"zs{first}", align_bytes=64)
-                values = z[:, (first - start) * PACK : (last - start) * PACK]
-                res = keep.tile([P, N // P, width], F32, name=f"res{first}", align_bytes=64)
-                shared = len(copies) > 1
-                acc = [
-                    psum.tile([P, N // P // len(copies), width], F32, name=f"acc{first}{n}", tag=f"bank{out_banks.pop(0)}")
-                    for n in range(len(copies))
-                ]
-                step = width // 2 if last == U else width
-                for at in range(0, width, step):
-                    part = slice(at, at + step)
-                    nc.vector.quantize_mx(
-                        out=z_words[:, part].bitcast(FP8X4),
-                        scales=z_scales[:, part],
-                        in_=values[:, at * PACK : (at + step) * PACK],
-                    )
-                    for block in range(N // P):
-                        cols = slice(block * P, (block + 1) * P)
-                        nc.tensor.matmul_mx(
-                            out=acc[block][:, 0, part] if shared else acc[0][:, block, part],
-                            lhsT=w3_c[:, cols].bitcast(FP8X4),
-                            lhsT_scale=w3_s[:, cols],
-                            rhs=z_words[:, part].bitcast(FP8X4),
-                            rhs_scale=z_scales[:, part],
-                            start=True,
-                            stop=True,
-                        )
-                filled.append((first, last, res, acc, copies))
-                first = last
-
-        def store():
-            while filled:
-                first, last, res, acc, copies = filled.pop(0)
-                for n, copy in enumerate(copies):
-                    part = slice(n, n + 1) if len(copies) > 1 else slice(0, N // P)
-                    copy(out=res[:, part], in_=acc[n][:])
-                    if last < U:
-                        nc.sync.dma_start(out=out_v[:, part, first:last], in_=res[:, part])
-                if last == U:
-                    nc.sync.dma_start(out=out_v[:, :, first:last], in_=res[:])
-
-        def join(u, t, start, first, last):
-            nc.vector.tensor_tensor(
-                out=u[:, t, first - start : last - start],
-                in0=e_all[t][:].indirect(entries(src_t, first, last)),
-                in1=fetched[t][:, first:last],
-                op=ADD,
+        def silu(z, start, first, last):
+            nc.scalar.activation(
+                out=z[:, (first - start) * PACK : (last - start) * PACK].rearrange(
+                    "p (c i t) -> p c t i", i=PACK, t=PACK
+                ),
+                in_=sums_of(slice(0, PACK), first, last).rearrange("p t (c i) -> p c t i", i=PACK),
+                func=SILU,
             )
 
-        out_banks, waiting, first = [4, 5, 2, 3, 0, 1, 6], None, 0
-        for u, widths in zip(places, EDGE_SLICES):
-            last = first + sum(widths)
-            for t in range(PACK - 1):
-                join(u, t, first, first, last)
-            if last == U:
-                finish(*waiting, (on_vector, on_scalar))
-                waiting = None
-            z = keep.tile([P, (last - first) * PACK], BF16, name=f"z{first}", align_bytes=64)
-            at = 0
-            for width in widths if last < U else (widths[0] // 2,) * 2:
-                join(u, PACK - 1, first, first + at, first + at + width)
-                nc.scalar.activation(
-                    out=z[:, at * PACK : (at + width) * PACK].rearrange("p (c i t) -> p c t i", i=PACK, t=PACK),
-                    in_=u[:, :, at : at + width].rearrange("p t (c i) -> p c t i", i=PACK),
-                    func=SILU,
+        def multiply(first, last, z, step, shared):
+            width = last - first
+            z_words = keep.tile([P, width], U32, name=f"zc{first}", align_bytes=64)
+            z_scales = keep.tile([P, width], U8, name=f"zs{first}", align_bytes=64)
+            count = blocks if shared else 1
+            acc = [
+                psum.tile([P, blocks // count, width], F32, name=f"acc{first}{n}", tag=f"bank{out_banks.pop(0)}")
+                for n in range(count)
+            ]
+            for at in range(0, width, step):
+                part = slice(at, at + step)
+                nc.vector.quantize_mx(
+                    out=z_words[:, part].bitcast(FP8X4),
+                    scales=z_scales[:, part],
+                    in_=z[:, at * PACK : (at + step) * PACK],
                 )
-                at += width
-            if waiting:
-                finish(*waiting)
-            store()
-            waiting = first, widths, z
-            first = last
-        finish(*waiting, (on_vector, on_scalar))
-        store()
+                for block in range(blocks):
+                    cols = slice(block * P, (block + 1) * P)
+                    nc.tensor.matmul_mx(
+                        out=acc[block][:, 0, part] if shared else acc[0][:, block, part],
+                        lhsT=w3_c[:, cols].bitcast(FP8X4),
+                        lhsT_scale=w3_s[:, cols],
+                        rhs=z_words[:, part].bitcast(FP8X4),
+                        rhs_scale=z_scales[:, part],
+                        start=True,
+                        stop=True,
+                    )
+            return acc
+
+        def store(first, last, acc, copies):
+            tag = f"z{last}" if last <= U // 2 else f"res{first}"
+            res = keep.tile([P, blocks, last - first], F32, name=f"res{first}", tag=tag, align_bytes=64)
+            for n, copy in enumerate(copies):
+                part = slice(n, n + 1) if len(copies) > 1 else slice(0, blocks)
+                copy(out=res[:, part], in_=acc[n][:])
+            nc.sync.dma_start(out=out_v[:, :, first:last], in_=res[:])
+
+        bounds = [sum(PIECES[:n]) for n in range(len(PIECES) + 1)]
+        spans = list(zip(bounds, bounds[1:]))
+        zs, accs = [], []
+
+        def step_of(first, last):
+            return (last - first) // 2 if last == U else last - first
+
+        def activate(n):
+            first, last = spans[n]
+            zs.append(keep.tile([P, (last - first) * PACK], BF16, name=f"z{first}", tag=f"z{first}", align_bytes=64))
+            join(PACK - 1, first, last)
+            for at in range(first, last, step_of(first, last)):
+                silu(zs[n], first, at, at + step_of(first, last))
+
+        def product(n):
+            first, last = spans[n]
+            accs.append(multiply(first, last, zs[n], step_of(first, last), last == U))
+
+        activate(0)
+        activate(1)
+        join(2, U // 2, U)
+        activate(2)
+        product(0)
+        activate(3)
+        activate(4)
+        for n in range(1, len(PIECES)):
+            product(n)
+        for n, copies in enumerate(((on_vector,), (on_vector,), (on_scalar,), (on_vector,), (on_vector, on_scalar))):
+            store(*spans[n], accs[n], copies)

@@ -255,7 +255,8 @@ def tile_picked_hub_silu_p_kernel(
         for n in range(PAIR):
             codes[Y, 1, PAIR + n], scales[Y, 1, PAIR + n] = codes[Y, 0, PACK + n], scales[Y, 0, PACK + n]
         empty_tile(Y, 0, on_vector)
-        empty_tile(Y, 1, on_vector)
+        empty_bank(Y, 1, 0, on_vector)
+        empty_bank(Y, 1, 1)
         for t in range(PAIR, PACK):
             for h in range(HALVES):
                 for g in range(PASSES):

@@ -181,7 +181,13 @@ def tile_picked_hub_silu_p_kernel(
             for h in range(HALVES):
                 empty_bank(a, t, h, copy)
 
-        fetched = {}
+        fetched, halves = {}, {}
+
+        def fetch_half(t, h, place):
+            halves[t, h] = place
+            nc.scalar.activation(
+                out=place, in_=e_all[t][:].indirect(entries(dst_t, h * U // 2, (h + 1) * U // 2)), func=COPY
+            )
 
         def fetch_sources(t, first=0, last=U, tag=None):
             if first == 0:
@@ -242,7 +248,7 @@ def tile_picked_hub_silu_p_kernel(
         fetch_sources(1)
         empty_bank(E, 2, 0, on_vector)
         empty_bank(E, 2, 1)
-        fetch_sources(2)
+        fetch_half(2, 0, keep.tile([P, U // 2], F32, name="third_early", align_bytes=64)[:])
         quantise(Y, 0, 0, lower)
         product_pair(Y, 0, 0)
         upper = woven_tile(Y, 0, PAIR, PASSES * PAIR)
@@ -257,6 +263,9 @@ def tile_picked_hub_silu_p_kernel(
         empty_tile(Y, 0, on_vector)
         empty_bank(Y, 1, 0, on_vector)
         empty_bank(Y, 1, 1)
+        e_all.append(keep.tile([P, S], F32, name="e_all3", tag="codes110", align_bytes=64))
+        results[E, 3] = e_all[3][:]
+        empty_tile(E, 3, on_scalar)
         for t in range(PAIR, PACK):
             for h in range(HALVES):
                 for g in range(PASSES):
@@ -272,7 +281,7 @@ def tile_picked_hub_silu_p_kernel(
 
         def join(t, first, last):
             h = first // (U // 2)
-            other = parked[h][:, first - h * U // 2 : last - h * U // 2] if t == PACK - 1 else fetched[t][:, first:last]
+            other = halves[t, h][:, first - h * U // 2 : last - h * U // 2] if t >= PAIR else fetched[t][:, first:last]
             nc.vector.tensor_tensor(
                 out=sums_of(t, first, last),
                 in0=y_all[t][:].indirect(entries(src_t, first, last)),
@@ -284,15 +293,9 @@ def tile_picked_hub_silu_p_kernel(
             join(t, 0, U // 2)
             join(t, U // 2, U)
         join(2, 0, U // 2)
-        e_all.append(keep.tile([P, S], F32, name="e_all3", tag="codes102", align_bytes=64))
-        results[E, 3] = e_all[3][:]
-        empty_tile(E, 3, on_scalar)
-        last_fetched = keep.tile([P, U // 2], F32, name="last_fetched", align_bytes=64)
-        parked = (sums_of(2, U // 2, U), last_fetched[:])
-        for h in range(2):
-            nc.scalar.activation(
-                out=parked[h], in_=e_all[3][:].indirect(entries(dst_t, h * U // 2, (h + 1) * U // 2)), func=COPY
-            )
+        fetch_half(3, 0, sums_of(2, U // 2, U))
+        fetch_half(2, 1, keep.tile([P, U // 2], F32, name="third_late", tag="scales102", align_bytes=64)[:])
+        fetch_half(3, 1, keep.tile([P, U // 2], F32, name="last_late", tag="codes102", align_bytes=64)[:])
 
         w3_s = planes[Y, 1, 0]
         for q in range(P // QUADRANT):
@@ -302,7 +305,7 @@ def tile_picked_hub_silu_p_kernel(
             )
 
         out_v = out.rearrange("(mt p) r -> p mt r", p=P)
-        out_banks = [2, 3, 4, 0, 5, 7]
+        out_banks = [2, 3, 4, 0, 5, 7, 1]
         blocks = N // P
 
         def silu(z, start, first, last):
@@ -346,10 +349,14 @@ def tile_picked_hub_silu_p_kernel(
         def store(first, last, acc, copies):
             tag = f"z{last}" if last <= U // 2 else f"res{first}"
             res = keep.tile([P, blocks, last - first], F32, name=f"res{first}", tag=tag, align_bytes=64)
+            wide = last - first == PIECES[0]
             for n, copy in enumerate(copies):
                 part = slice(n, n + 1) if len(copies) > 1 else slice(0, blocks)
-                copy(out=res[:, part], in_=acc[n][:])
-            nc.sync.dma_start(out=out_v[:, :, first:last], in_=res[:])
+                copy(out=res[:, part], in_=acc[n][:] if len(acc) == len(copies) else acc[0][:, part])
+                if wide:
+                    nc.sync.dma_start(out=out_v[:, part, first:last], in_=res[:, part])
+            if not wide:
+                nc.sync.dma_start(out=out_v[:, :, first:last], in_=res[:])
 
         bounds = [sum(PIECES[:n]) for n in range(len(PIECES) + 1)]
         spans = list(zip(bounds, bounds[1:]))
@@ -367,7 +374,7 @@ def tile_picked_hub_silu_p_kernel(
 
         def product(n):
             first, last = spans[n]
-            accs.append(multiply(first, last, zs[n], step_of(first, last), last == U))
+            accs.append(multiply(first, last, zs[n], step_of(first, last), n in (2, 4)))
 
         activate(0)
         activate(1)
@@ -378,5 +385,5 @@ def tile_picked_hub_silu_p_kernel(
         activate(4)
         for n in range(1, len(PIECES)):
             product(n)
-        for n, copies in enumerate(((on_vector,), (on_vector,), (on_scalar,), (on_vector,), (on_vector, on_scalar))):
+        for n, copies in enumerate(((on_vector,) * 2, (on_vector,) * 2, (on_scalar,) * 2, (on_vector,), (on_vector, on_scalar))):
             store(*spans[n], accs[n], copies)

@@ -311,9 +311,9 @@ def tile_picked_hub_silu_p_kernel(
         def silu(z, start, first, last):
             nc.scalar.activation(
                 out=z[:, (first - start) * PACK : (last - start) * PACK].rearrange(
-                    "p (c i t) -> p c t i", i=PACK, t=PACK
+                    "p (c i t) -> p c t i", i=PAIR, t=PACK
                 ),
-                in_=sums_of(slice(0, PACK), first, last).rearrange("p t (c i) -> p c t i", i=PACK),
+                in_=sums_of(slice(0, PACK), first, last).rearrange("p t (c i) -> p c t i", i=PAIR),
                 func=SILU,
             )
 

@@ -17,23 +17,39 @@ SILU = mybir.ActivationFunctionType.Silu
 COPY = mybir.ActivationFunctionType.Copy
 
 P = 128
-HALF = P // 2
 PACK = 4
 PAIR = 2
 K_PASS = P * PACK
 PASSES = K // K_PASS
 BANK = 512
 HALVES = S // BANK
+QUARTER = S // 4
 LIST_ROWS = 16
 QUADRANT = 32
 SCALE_ROWS = 4
+BLOCKS = N // P
+HALF_EDGES = U // 2
 E, Y = 0, 1
 
-WINDOW = S + LIST_ROWS
+WIDE_WINDOW = S + LIST_ROWS
 
-PIECES = (256, 256, 256, 128, 128)
-LATE_PIECES = ((0, 96), (96, 128))
-TILE_BANKS = ((None, (2, 3), (4, 0), (1, 6)), ((5, 7), (2, 3), (4, 0), (5, 7)))
+LATE_PIECES = ((0, 96), (96, P))
+SCALAR_SHARE = 64
+
+WIDE = 256
+PIECES = (WIDE, WIDE, WIDE, WIDE // 2, WIDE // 2)
+
+QUARTER_BANKS = (0, 1, 6, 7)
+TILE_BANKS = {
+    (E, 1): (2, 3),
+    (E, 2): (4, 0),
+    (E, 3): (1, 6),
+    (Y, 0): (5, 7),
+    (Y, 1): (2, 3),
+    (Y, 2): (4, 0),
+    (Y, 3): (5, 7),
+}
+RESULT_BANKS = ((2,), (3, 6), (4, 0), (5,), (7, 1))
 
 
 def entries(list_tile, first, last):
@@ -50,340 +66,313 @@ def tile_picked_hub_silu_p_kernel(
         keep = ctx.enter_context(tc.tile_pool(name="keep", bufs=1))
         psum = ctx.enter_context(tc.psum_pool(name="psum", bufs=1))
 
+        def sbuf(name, shape, dtype, tag=None):
+            return keep.tile(shape, dtype, name=name, tag=tag or name, align_bytes=64)
+
+        def multiply(acc, stationary, moving, start=True, stop=True):
+            nc.tensor.matmul_mx(
+                out=acc,
+                lhsT=stationary[0].bitcast(FP8X4),
+                lhsT_scale=stationary[1],
+                rhs=moving[0].bitcast(FP8X4),
+                rhs_scale=moving[1],
+                start=start,
+                stop=stop,
+            )
+
         offs_t = lists.tile([P, S // LIST_ROWS], U16, name="offs_t")
         src_t = lists.tile([P, U // LIST_ROWS], U16, name="src_t")
         dst_t = lists.tile([P, U // LIST_ROWS], U16, name="dst_t")
 
-        xs_all = keep.tile([P, T], U8, name="xs_all", tag="xs_all", align_bytes=64)
-        xs = [keep.tile([P, S], U8, name=f"xs{g}", align_bytes=64) for g in range(PASSES)]
+        xs_all = sbuf("xs_all", [P, T], U8)
+        xs = [sbuf(f"xs{g}", [P, S], U8) for g in range(PASSES)]
         nc.vector.memset(xs_all[QUADRANT : 2 * QUADRANT].bitcast(I32), 0)
         nc.vector.memset(xs_all[2 * QUADRANT :].bitcast(I32), 0)
         for g in range(PASSES):
             nc.gpsimd.memset(xs[g][:].bitcast(I32), 0)
 
-        xw_all = {}
-        raw = {}
+        xw_all, xw, raw, late = {}, {}, {}, []
 
-        def load_words(g, tag):
-            xw_all[g] = keep.tile([P, T], U32, name=f"xw_all{g}", tag=tag, align_bytes=64)
+        def load_words(g):
+            xw_all[g] = sbuf(f"xw_all{g}", [P, T], U32)
             nc.sync.dma_start(
                 out=xw_all[g][:].bitcast(I32), in_=x_words[g].rearrange("p n t -> p (n t)").bitcast(I32)
             )
 
-        def load_weight(a, g, tag):
-            raw[a, g] = keep.tile([P, PACK, H], F32, name=f"raw{a}{g}", tag=tag, align_bytes=64)
-            k_rows = (w2, w1)[a][g * K_PASS : (g + 1) * K_PASS, :]
-            nc.sync.dma_start(out=raw[a, g][:], in_=k_rows.rearrange("(p j) c -> p j c", j=PACK))
+        def rows_of(a, g):
+            return (w2, w1)[a][g * K_PASS : (g + 1) * K_PASS, :].rearrange("(p j) c -> p j c", j=PACK)
 
-        nc.sync.dma_start(offs_t[:], offs)
-        nc.sync.dma_start(out=xs_all[:QUADRANT, :].bitcast(I32), in_=x_scales.rearrange("g r n -> (g r) n").bitcast(I32))
-        load_words(0, "xw_all0")
-        load_weight(E, 0, "raw00")
-        load_words(1, "xw_all1")
-        nc.sync.dma_start(src_t[:], src)
-        nc.sync.dma_start(dst_t[:], dst)
-        late_rows = w2[K_PASS:, :].rearrange("(p j) c -> p j c", j=PACK)
-        late = []
+        def load_weight(a, g, tag=None):
+            raw[a, g] = sbuf(f"raw{a}{g}", [P, PACK, H], F32, tag)
+            nc.sync.dma_start(out=raw[a, g][:], in_=rows_of(a, g))
 
         def load_late(tag):
             m0, m1 = LATE_PIECES[len(late)]
-            late.append(keep.tile([P, PACK, PACK * (m1 - m0)], F32, name=f"late{m0}", tag=tag, align_bytes=64))
-            nc.sync.dma_start(out=late[-1][:], in_=late_rows[:, :, PACK * m0 : PACK * m1])
+            late.append(sbuf(f"late{m0}", [P, PACK, PACK * (m1 - m0)], F32, tag))
+            nc.sync.dma_start(out=late[-1][:], in_=rows_of(E, 1)[:, :, PACK * m0 : PACK * m1])
 
-        picked = keep.tile([P, S], U8, name="picked", tag="picked", align_bytes=64)
-        xw = {}
-        codes, scales, planes = {}, {}, {}
+        nc.sync.dma_start(offs_t[:], offs)
+        nc.sync.dma_start(
+            out=xs_all[:QUADRANT, :].bitcast(I32), in_=x_scales.rearrange("g r n -> (g r) n").bitcast(I32)
+        )
+        load_words(0)
+        load_weight(E, 0)
+        load_words(1)
+        nc.sync.dma_start(src_t[:], src)
+        nc.sync.dma_start(dst_t[:], dst)
 
-        def gather_words(g, tag):
-            xw[g] = keep.tile([P, S], U32, name=f"xw{g}", tag=tag, align_bytes=64)
+        picked_scales = sbuf("picked_scales", [P, S], U8)
+        weights, planes = {}, {}
+
+        def gather_words(g):
+            xw[g] = sbuf(f"xw{g}", [P, S], U32)
             nc.vector.tensor_copy(out=xw[g][:], in_=xw_all[g][:].indirect(offs_t[:]))
 
-        def woven_tile(a, g, first, count, tag=None):
-            name = f"woven{a}{g}{first}"
-            return keep.tile([P, count, P, PACK], BF16, name=name, tag=tag or name, align_bytes=64)
+        def woven_tile(name, count):
+            return sbuf(name, [P, count, P, PACK], BF16)
 
-        def weave(a, g, first, copy, woven):
-            dealt = raw[a, g][:].rearrange("p j (m t) -> p m j t", t=PACK)[:, :, :, first : first + PAIR]
-            copy(out=woven.rearrange("p t m j -> p m j t"), in_=dealt)
+        def weave(source, first, woven, copy, m0=0, m1=P, base=0):
+            dealt = source[:].rearrange("p j (m t) -> p m j t", t=PACK)[:, :, :, first : first + PAIR]
+            copy(out=woven.rearrange("p t m j -> p m j t")[:, m0:m1], in_=dealt[:, m0 - base : m1 - base])
 
-        def quantise(a, g, first, woven, tag=None):
-            count = woven.shape[1]
-            name = f"codes{a}{g}{first}"
-            words = keep.tile([P, count * P], U32, name=name, tag=tag or name, align_bytes=64)
-            plane = keep.tile([P, count * P], U8, name=f"scales{a}{g}{first}", tag=f"scales{a}{g}{first}", align_bytes=64)
-            nc.vector.quantize_mx(
-                out=words[:].bitcast(FP8X4), scales=plane[:], in_=woven[:, :].rearrange("p t m j -> p (t m j)")
-            )
-            planes[a, g, first] = plane
-            for n in range(count):
-                codes[a, g, first + n] = words[:, n * P : (n + 1) * P]
-                scales[a, g, first + n] = plane[:, n * P : (n + 1) * P]
-
-        def woven_pair(a, g, first, copy, tag=None):
-            woven = woven_tile(a, g, first, PAIR, tag)
-            weave(a, g, first, copy, woven[:])
+        def woven_pair(a, g, first, copy):
+            woven = woven_tile(f"woven{a}{g}{first}", PAIR)
+            weave(raw[a, g], first, woven[:], copy)
             return woven
 
-        def weave_late(first, woven, piece, m0, m1, copy):
-            dealt = late[piece][:].rearrange("p j (m t) -> p m j t", t=PACK)[:, :, :, first : first + PAIR]
-            base = LATE_PIECES[piece][0]
-            copy(out=woven[:].rearrange("p t m j -> p m j t")[:, m0:m1], in_=dealt[:, m0 - base : m1 - base])
+        def quantise(name, woven, keys):
+            words = sbuf(f"codes_{name}", [P, len(keys) * P], U32)
+            planes[name] = sbuf(f"plane_{name}", [P, len(keys) * P], U8)
+            nc.vector.quantize_mx(
+                out=words[:].bitcast(FP8X4), scales=planes[name][:], in_=woven[:, :].rearrange("p t m j -> p (t m j)")
+            )
+            for n, key in enumerate(keys):
+                weights[key] = words[:, n * P : (n + 1) * P], planes[name][:, n * P : (n + 1) * P]
+
+        def pair_keys(a, g, first):
+            return [(a, g, first + n) for n in range(PAIR)]
+
+        def one_pass(acc, a, g, t, columns):
+            multiply(acc[:], weights[a, g, t], (xw[g][:, columns], xs[g][:, columns]), g == 0, g == PASSES - 1)
 
         banks = {}
 
         def product_pass(a, g, t, h):
             if g == 0:
-                banks[a, t, h] = psum.tile([P, BANK], F32, name=f"bank{a}{t}{h}", tag=f"bank{TILE_BANKS[a][t][h]}")
-            picked = slice(h * BANK, (h + 1) * BANK)
-            nc.tensor.matmul_mx(
-                out=banks[a, t, h][:],
-                lhsT=codes[a, g, t].bitcast(FP8X4),
-                lhsT_scale=scales[a, g, t],
-                rhs=xw[g][:, picked].bitcast(FP8X4),
-                rhs_scale=xs[g][:, picked],
-                start=(g == 0),
-                stop=(g == PASSES - 1),
-            )
+                banks[a, t, h] = psum.tile([P, BANK], F32, name=f"acc{a}{t}{h}", tag=f"bank{TILE_BANKS[a, t][h]}")
+            one_pass(banks[a, t, h], a, g, t, slice(h * BANK, (h + 1) * BANK))
 
-        quarters = [psum.tile([P, BANK // 2], F32, name=f"quarter{n}", tag=f"bank{(0, 1, 6, 7)[n]}") for n in range(4)]
+        def both_passes(a, t, h):
+            for g in range(PASSES):
+                product_pass(a, g, t, h)
+
+        def lower_pair_pass(g):
+            for t in range(PAIR):
+                for h in range(HALVES):
+                    product_pass(Y, g, t, h)
+
+        quarters = [psum.tile([P, QUARTER], F32, name=f"quarter{b}", tag=f"bank{b}") for b in QUARTER_BANKS]
 
         def first_tile_pass(g):
-            for n in range(4):
-                picked = slice(n * BANK // 2, (n + 1) * BANK // 2)
-                nc.tensor.matmul_mx(
-                    out=quarters[n][:],
-                    lhsT=codes[E, g, 0].bitcast(FP8X4),
-                    lhsT_scale=scales[E, g, 0],
-                    rhs=xw[g][:, picked].bitcast(FP8X4),
-                    rhs_scale=xs[g][:, picked],
-                    start=(g == 0),
-                    stop=(g == PASSES - 1),
-                )
+            for n, acc in enumerate(quarters):
+                one_pass(acc, E, g, 0, slice(n * QUARTER, (n + 1) * QUARTER))
 
-        def product_pair(a, g, first):
-            for t in range(first, first + PAIR):
-                for h in range(HALVES):
-                    product_pass(a, g, t, h)
-
-        e_all = [keep.tile([P, WINDOW], F32, name=f"e_all{t}", align_bytes=64) for t in range(PACK - 1)]
-        for t in range(PACK - 1):
-            nc.gpsimd.memset(e_all[t][:, S:], 0.0)
+        e_all = [sbuf(f"e_all{t}", [P, WIDE_WINDOW], F32) for t in range(PAIR)]
+        for window in e_all:
+            nc.gpsimd.memset(window[:, S:], 0.0)
+        e_all.append(sbuf("e_all2", [P, S], F32))
         warm = keep.tile([P, 1], F32, name="warm")
         nc.scalar.activation(out=warm[:], in_=e_all[0][:, S : S + 1], func=SILU)
-        y_all = [keep.tile([P, S], F32, name=f"y_all{t}", align_bytes=64) for t in range(PACK)]
-        results = {(E, t): e_all[t][:, :S] for t in range(PACK - 1)}
-        results.update({(Y, t): y_all[t][:, :S] for t in range(PACK)})
+        y_all = [sbuf(f"y_all{t}", [P, S], F32) for t in range(PACK)]
 
-        def empty_bank(a, t, h, copy=on_scalar):
-            copy(out=results[a, t][:, h * BANK : (h + 1) * BANK], in_=banks[a, t, h][:])
+        def empty_bank(a, t, h, copy):
+            copy(out=(e_all, y_all)[a][t][:, h * BANK : (h + 1) * BANK], in_=banks[a, t, h][:])
 
-        def empty_tile(a, t, copy=on_scalar):
+        def empty_tile(a, t, copy):
             for h in range(HALVES):
                 empty_bank(a, t, h, copy)
 
-        fetched, halves = {}, {}
+        fetched = {}
 
-        def fetch_half(t, h, place):
-            halves[t, h] = place
-            nc.scalar.activation(
-                out=place, in_=e_all[t][:].indirect(entries(dst_t, h * U // 2, (h + 1) * U // 2)), func=COPY
-            )
-
-        def fetch_sources(t, first=0, last=U, tag=None):
-            if first == 0:
-                fetched[t] = keep.tile([P, U], F32, name=f"fetched{t}", tag=tag or f"fetched{t}", align_bytes=64)
-            nc.scalar.activation(
-                out=fetched[t][:, first:last], in_=e_all[t][:].indirect(entries(dst_t, first, last)), func=COPY
-            )
-
-        nc.vector.tensor_copy(out=picked[:], in_=xs_all[:].indirect(offs_t[:]))
-
+        def fetch(t, first, last, place):
+            nc.scalar.activation(out=place, in_=e_all[t][:].indirect(entries(dst_t, first, last)), func=COPY)
+            for at in range(first, last, HALF_EDGES):
+                fetched[t, at] = place[:, at - first : at - first + HALF_EDGES]
 
         def place_scale_rows(g):
             for q in range(P // QUADRANT):
                 to, at = QUADRANT * q, SCALE_ROWS * (P // QUADRANT * g + q)
                 nc.sync.dma_start(
-                    out=xs[g][to : to + SCALE_ROWS, :].bitcast(I32), in_=picked[at : at + SCALE_ROWS, :].bitcast(I32)
+                    out=xs[g][to : to + SCALE_ROWS, :].bitcast(I32),
+                    in_=picked_scales[at : at + SCALE_ROWS, :].bitcast(I32),
                 )
 
+        nc.vector.tensor_copy(out=picked_scales[:], in_=xs_all[:].indirect(offs_t[:]))
         place_scale_rows(0)
-        gather_words(0, "xw0")
+        gather_words(0)
         load_late("xs_all")
         load_late("xw_all0")
         place_scale_rows(1)
-        early = woven_pair(E, 0, 0, on_scalar)
-        quantise(E, 0, PAIR, woven_pair(E, 0, PAIR, on_vector))
-        quantise(E, 0, 0, early)
-        load_weight(Y, 0, "raw00")
-        gather_words(1, "xw1")
+        e_lower = woven_pair(E, 0, 0, on_scalar)
+        quantise("e0_upper", woven_pair(E, 0, PAIR, on_vector), pair_keys(E, 0, PAIR))
+        quantise("e0_lower", e_lower, pair_keys(E, 0, 0))
+        load_weight(Y, 0, f"raw{E}0")
+        gather_words(1)
         load_weight(Y, 1, "xw_all1")
         first_tile_pass(0)
         for t, h in ((1, 0), (1, 1), (2, 0)):
             product_pass(E, 0, t, h)
-        lower, upper = woven_tile(E, 1, 0, PAIR), woven_tile(E, 1, PAIR, PAIR)
-        cut = LATE_PIECES[0][1]
-        weave_late(0, lower, 0, 0, cut, on_scalar)
-        weave_late(0, lower, 1, cut, P, on_vector)
-        quantise(E, 1, 0, lower[:, :1])
+
+        late_lower, late_upper = woven_tile("late_lower", PAIR), woven_tile("late_upper", PAIR)
+        cut = LATE_PIECES[1][0]
+        weave(late[0], 0, late_lower[:], on_scalar, 0, cut)
+        weave(late[1], 0, late_lower[:], on_vector, cut, P, cut)
+        quantise("e1_tile0", late_lower[:, :1], [(E, 1, 0)])
         first_tile_pass(1)
-        quantise(E, 1, 1, lower[:, 1:])
+        quantise("e1_tile1", late_lower[:, 1:], [(E, 1, 1)])
         for h in range(HALVES):
             product_pass(E, 1, 1, h)
-        weave_late(PAIR, upper, 0, 0, P // 2, on_scalar)
-        weave_late(PAIR, upper, 1, cut, P, on_vector)
-        weave_late(PAIR, upper, 0, P // 2, cut, on_vector)
-        for n in range(4):
+        weave(late[0], PAIR, late_upper[:], on_scalar, 0, SCALAR_SHARE)
+        weave(late[1], PAIR, late_upper[:], on_vector, cut, P, cut)
+        weave(late[0], PAIR, late_upper[:], on_vector, SCALAR_SHARE, cut)
+        for n, acc in enumerate(quarters):
             copy = on_vector if n % 2 else on_scalar
-            copy(out=results[E, 0][:, n * BANK // 2 : (n + 1) * BANK // 2], in_=quarters[n][:])
-        w3_c = keep.tile([P, N], U32, name="w3_c", tag="xs_all", align_bytes=64)
-        nc.sync.dma_start(out=w3_c[:].bitcast(I32), in_=w3_words[0].rearrange("p n t -> p (n t)").bitcast(I32))
-        quantise(E, 1, PAIR, upper)
-        fetch_sources(0)
+            copy(out=e_all[0][:, n * QUARTER : (n + 1) * QUARTER], in_=acc[:])
+        w3_codes = sbuf("w3_codes", [P, N], U32, "xs_all")
+        nc.sync.dma_start(out=w3_codes[:].bitcast(I32), in_=w3_words[0].rearrange("p n t -> p (n t)").bitcast(I32))
+        quantise("e1_upper", late_upper, pair_keys(E, 1, PAIR))
+        fetch(0, 0, U, sbuf("fetched0", [P, U], F32)[:])
         product_pass(E, 1, 2, 0)
         for t, h in ((2, 1), (3, 0), (3, 1)):
-            for g in range(PASSES):
-                product_pass(E, g, t, h)
+            both_passes(E, t, h)
+
         empty_tile(E, 1, on_vector)
-        lower = woven_pair(Y, 0, 0, on_vector)
-        fetch_sources(1)
+        y_lower = woven_pair(Y, 0, 0, on_vector)
+        fetch(1, 0, U, sbuf("fetched1", [P, U], F32)[:])
         empty_bank(E, 2, 0, on_vector)
-        empty_bank(E, 2, 1)
-        fetch_half(2, 0, keep.tile([P, U // 2], F32, name="third_early", align_bytes=64)[:])
-        quantise(Y, 0, 0, lower)
-        product_pair(Y, 0, 0)
-        upper = woven_tile(Y, 0, PAIR, PASSES * PAIR)
-        weave(Y, 0, PAIR, on_vector, upper[:, :PAIR])
-        lower = woven_pair(Y, 1, 0, on_vector)
-        weave(Y, 1, PAIR, on_vector, upper[:, PAIR:])
-        quantise(Y, 1, 0, lower)
-        product_pair(Y, 1, 0)
-        quantise(Y, 0, PAIR, upper)
-        for n in range(PAIR):
-            codes[Y, 1, PAIR + n], scales[Y, 1, PAIR + n] = codes[Y, 0, PACK + n], scales[Y, 0, PACK + n]
+        empty_bank(E, 2, 1, on_scalar)
+        fetch(2, 0, HALF_EDGES, sbuf("fetched2_early", [P, HALF_EDGES], F32)[:])
+        quantise("y0_lower", y_lower, pair_keys(Y, 0, 0))
+        lower_pair_pass(0)
+        y_upper = woven_tile("y_upper", PASSES * PAIR)
+        weave(raw[Y, 0], PAIR, y_upper[:, :PAIR], on_vector)
+        y_lower = woven_pair(Y, 1, 0, on_vector)
+        weave(raw[Y, 1], PAIR, y_upper[:, PAIR:], on_vector)
+        quantise("y1_lower", y_lower, pair_keys(Y, 1, 0))
+        lower_pair_pass(1)
+        quantise("y_upper", y_upper, pair_keys(Y, 0, PAIR) + pair_keys(Y, 1, PAIR))
         empty_tile(Y, 0, on_vector)
         empty_bank(Y, 1, 0, on_vector)
-        empty_bank(Y, 1, 1)
-        e_all.append(keep.tile([P, S], F32, name="e_all3", tag="codes110", align_bytes=64))
-        results[E, 3] = e_all[3][:]
+        empty_bank(Y, 1, 1, on_scalar)
+        e_all.append(sbuf("e_all3", [P, S], F32, "codes_y1_lower"))
         empty_tile(E, 3, on_scalar)
         for t in range(PAIR, PACK):
             for h in range(HALVES):
-                for g in range(PASSES):
-                    product_pass(Y, g, t, h)
-            empty_tile(Y, t)
-        sums = keep.tile([P, PACK * U - PIECES[0]], F32, name="sums", align_bytes=64)
-        early_sums, late_sums = sums[:, PACK * U // 2 - PIECES[0] :], sums[:, : PACK * U // 2]
-        u = [half.rearrange("p (t r) -> p t r", t=PACK) for half in (early_sums, late_sums)]
+                both_passes(Y, t, h)
+            empty_tile(Y, t, on_scalar)
+
+        sums = sbuf("sums", [P, PACK * U - WIDE], F32)
+        sums_by_half = [
+            half.rearrange("p (t r) -> p t r", t=PACK)
+            for half in (sums[:, PACK * HALF_EDGES - WIDE :], sums[:, : PACK * HALF_EDGES])
+        ]
 
         def sums_of(t, first, last):
-            h = first // (U // 2)
-            return u[h][:, t, first - h * U // 2 : last - h * U // 2]
+            h, at = divmod(first, HALF_EDGES)
+            return sums_by_half[h][:, t, at : at + last - first]
 
         def join(t, first, last):
-            h = first // (U // 2)
-            other = halves[t, h][:, first - h * U // 2 : last - h * U // 2] if t >= PAIR else fetched[t][:, first:last]
+            at = first % HALF_EDGES
             nc.vector.tensor_tensor(
                 out=sums_of(t, first, last),
                 in0=y_all[t][:].indirect(entries(src_t, first, last)),
-                in1=other,
+                in1=fetched[t, first - at][:, at : at + last - first],
                 op=ADD,
             )
 
         for t in range(PAIR):
-            join(t, 0, U // 2)
-            join(t, U // 2, U)
-        join(2, 0, U // 2)
-        fetch_half(3, 0, sums_of(2, U // 2, U))
-        fetch_half(2, 1, keep.tile([P, U // 2], F32, name="third_late", tag="scales102", align_bytes=64)[:])
-        fetch_half(3, 1, keep.tile([P, U // 2], F32, name="last_late", tag="codes102", align_bytes=64)[:])
+            join(t, 0, HALF_EDGES)
+            join(t, HALF_EDGES, U)
+        join(2, 0, HALF_EDGES)
+        fetch(3, 0, HALF_EDGES, sums_of(2, HALF_EDGES, U))
+        fetch(2, HALF_EDGES, U, sbuf("fetched2_late", [P, HALF_EDGES], F32, "plane_y_upper")[:])
+        fetch(3, HALF_EDGES, U, sbuf("fetched3_late", [P, HALF_EDGES], F32, "codes_y_upper")[:])
 
-        w3_s = planes[Y, 1, 0]
+        w3_plane = planes["y1_lower"]
         for q in range(P // QUADRANT):
             nc.sync.dma_start(
-                out=w3_s[QUADRANT * q : QUADRANT * q + SCALE_ROWS, :].bitcast(I32),
+                out=w3_plane[QUADRANT * q : QUADRANT * q + SCALE_ROWS, :].bitcast(I32),
                 in_=w3_scales[0, SCALE_ROWS * q : SCALE_ROWS * (q + 1), :].bitcast(I32),
             )
 
-        out_v = out.rearrange("(mt p) r -> p mt r", p=P)
-        out_banks = [2, 3, 4, 0, 5, 7, 1]
-        blocks = N // P
+        out_v = out.rearrange("(b p) r -> p b r", p=P)
+        spans = [(sum(PIECES[:n]), sum(PIECES[: n + 1])) for n in range(len(PIECES))]
+        z, results = [], []
 
-        def silu(z, start, first, last):
-            nc.scalar.activation(
-                out=z[:, (first - start) * PACK : (last - start) * PACK].rearrange(
-                    "p (c i t) -> p c t i", i=PAIR, t=PACK
-                ),
-                in_=sums_of(slice(0, PACK), first, last).rearrange("p t (c i) -> p c t i", i=PAIR),
-                func=SILU,
-            )
-
-        def multiply(first, last, z, step, shared):
-            width = last - first
-            z_words = keep.tile([P, width], U32, name=f"zc{first}", align_bytes=64)
-            z_scales = keep.tile([P, width], U8, name=f"zs{first}", align_bytes=64)
-            count = blocks if shared else 1
-            acc = [
-                psum.tile([P, blocks // count, width], F32, name=f"acc{first}{n}", tag=f"bank{out_banks.pop(0)}")
-                for n in range(count)
-            ]
-            for at in range(0, width, step):
-                part = slice(at, at + step)
-                nc.vector.quantize_mx(
-                    out=z_words[:, part].bitcast(FP8X4),
-                    scales=z_scales[:, part],
-                    in_=z[:, at * PACK : (at + step) * PACK],
-                )
-                for block in range(blocks):
-                    cols = slice(block * P, (block + 1) * P)
-                    nc.tensor.matmul_mx(
-                        out=acc[block][:, 0, part] if shared else acc[0][:, block, part],
-                        lhsT=w3_c[:, cols].bitcast(FP8X4),
-                        lhsT_scale=w3_s[:, cols],
-                        rhs=z_words[:, part].bitcast(FP8X4),
-                        rhs_scale=z_scales[:, part],
-                        start=True,
-                        stop=True,
-                    )
-            return acc
-
-        def store(first, last, acc, copies):
-            tag = f"z{last}" if last <= U // 2 else f"res{first}"
-            res = keep.tile([P, blocks, last - first], F32, name=f"res{first}", tag=tag, align_bytes=64)
-            wide = last - first == PIECES[0]
-            for n, copy in enumerate(copies):
-                part = slice(n, n + 1) if len(copies) > 1 else slice(0, blocks)
-                copy(out=res[:, part], in_=acc[n][:] if len(acc) == len(copies) else acc[0][:, part])
-                if wide:
-                    nc.sync.dma_start(out=out_v[:, part, first:last], in_=res[:, part])
-            if not wide:
-                nc.sync.dma_start(out=out_v[:, :, first:last], in_=res[:])
-
-        bounds = [sum(PIECES[:n]) for n in range(len(PIECES) + 1)]
-        spans = list(zip(bounds, bounds[1:]))
-        zs, accs = [], []
-
-        def step_of(first, last):
-            return (last - first) // 2 if last == U else last - first
+        def parts(n):
+            step = PIECES[n] // 2 if spans[n][1] == U else PIECES[n]
+            return [slice(at, at + step) for at in range(0, PIECES[n], step)]
 
         def activate(n):
-            first, last = spans[n]
-            zs.append(keep.tile([P, (last - first) * PACK], BF16, name=f"z{first}", tag=f"z{first}", align_bytes=64))
-            join(PACK - 1, first, last)
-            for at in range(first, last, step_of(first, last)):
-                silu(zs[n], first, at, at + step_of(first, last))
+            first = spans[n][0]
+            z.append(sbuf(f"z{first}", [P, PIECES[n] * PACK], BF16))
+            if first % WIDE == 0:
+                join(PACK - 1, first, first + WIDE)
+            for part in parts(n):
+                nc.scalar.activation(
+                    out=z[n][:, part.start * PACK : part.stop * PACK].rearrange("p (c i t) -> p c t i", i=PAIR, t=PACK),
+                    in_=sums_of(slice(0, PACK), first + part.start, first + part.stop).rearrange(
+                        "p t (c i) -> p c t i", i=PAIR
+                    ),
+                    func=SILU,
+                )
 
         def product(n):
+            first, width = spans[n][0], PIECES[n]
+            z_codes, z_plane = sbuf(f"z_codes{first}", [P, width], U32), sbuf(f"z_plane{first}", [P, width], U8)
+            in_a_bank = BLOCKS // len(RESULT_BANKS[n])
+            accs = [
+                psum.tile([P, in_a_bank, width], F32, name=f"result{first}_{b}", tag=f"bank{b}") for b in RESULT_BANKS[n]
+            ]
+            results.append(accs)
+            for part in parts(n):
+                nc.vector.quantize_mx(
+                    out=z_codes[:, part].bitcast(FP8X4),
+                    scales=z_plane[:, part],
+                    in_=z[n][:, part.start * PACK : part.stop * PACK],
+                )
+                for b in range(BLOCKS):
+                    cols = slice(b * P, (b + 1) * P)
+                    multiply(
+                        accs[b // in_a_bank][:, b % in_a_bank, part],
+                        (w3_codes[:, cols], w3_plane[:, cols]),
+                        (z_codes[:, part], z_plane[:, part]),
+                    )
+
+        def store(n, copies):
             first, last = spans[n]
-            accs.append(multiply(first, last, zs[n], step_of(first, last), n in (2, 4)))
+            staged = sbuf(f"staged{first}", [P, BLOCKS, last - first], F32, f"z{last}" if last <= HALF_EDGES else None)
+            in_a_bank, in_a_copy = BLOCKS // len(results[n]), BLOCKS // len(copies)
+            for c, copy in enumerate(copies):
+                rows = slice(c * in_a_copy, (c + 1) * in_a_copy)
+                at = rows.start % in_a_bank
+                copy(out=staged[:, rows], in_=results[n][rows.start // in_a_bank][:, at : at + in_a_copy])
+                if PIECES[n] == WIDE:
+                    nc.sync.dma_start(out=out_v[:, rows, first:last], in_=staged[:, rows])
+            if PIECES[n] < WIDE:
+                nc.sync.dma_start(out=out_v[:, :, first:last], in_=staged[:])
 
         activate(0)
         activate(1)
-        join(2, U // 2, U)
+        join(2, HALF_EDGES, U)
         activate(2)
         product(0)
         activate(3)
         activate(4)
         for n in range(1, len(PIECES)):
             product(n)
-        for n, copies in enumerate(((on_vector,) * 2, (on_vector,) * 2, (on_scalar,) * 2, (on_vector,), (on_vector, on_scalar))):
-            store(*spans[n], accs[n], copies)
+        store(0, (on_vector, on_vector))
+        store(1, (on_vector, on_scalar))
+        store(2, (on_scalar, on_scalar))
+        store(3, (on_vector,))
+        store(4, (on_vector, on_scalar))

from contextlib import ExitStack

import concourse.mybir as mybir

K, T, S, H, N, U = 1024, 2048, 1024, 512, 256, 1024
FLOPS = 2 * (2 * K * H * S + H * N * U)

F32 = mybir.dt.float32
BF16 = mybir.dt.bfloat16
I32 = mybir.dt.int32
U32 = mybir.dt.uint32
U16 = mybir.dt.uint16
U8 = mybir.dt.uint8
FP8X4 = mybir.dt.float8_e4m3fn_x4
ADD = mybir.AluOpType.add
SILU = mybir.ActivationFunctionType.Silu
COPY = mybir.ActivationFunctionType.Copy

P = 128
PACK = 4
PAIR = 2
K_PASS = P * PACK
PASSES = K // K_PASS
BANK = 512
HALVES = S // BANK
QUARTER = S // 4
LIST_ROWS = 16
QUADRANT = 32
SCALE_ROWS = 4
BLOCKS = N // P
HALF_EDGES = U // 2
E, Y = 0, 1

WIDE_WINDOW = S + LIST_ROWS

LATE_PIECES = ((0, 96), (96, P))
SCALAR_SHARE = 64

WIDE = 256
PIECES = (WIDE, WIDE, WIDE, WIDE // 2, WIDE // 2)

QUARTER_BANKS = (0, 1, 6, 7)
TILE_BANKS = {
    (E, 1): (2, 3),
    (E, 2): (4, 0),
    (E, 3): (1, 6),
    (Y, 0): (5, 7),
    (Y, 1): (2, 3),
    (Y, 2): (4, 0),
    (Y, 3): (5, 7),
}
RESULT_BANKS = ((2,), (3, 6), (4, 0), (5,), (7, 1))


def entries(list_tile, first, last):
    return list_tile[:, first // LIST_ROWS : last // LIST_ROWS]


def tile_picked_hub_silu_p_kernel(
    tc, x_words, x_scales, w1, w2, w3_words, w3_scales, offs, src, dst, out
):
    nc = tc.nc
    on_scalar, on_vector = nc.scalar.copy, nc.vector.tensor_copy
    with ExitStack() as ctx:
        lists = ctx.enter_context(tc.tile_pool(name="lists", bufs=1))
        keep = ctx.enter_context(tc.tile_pool(name="keep", bufs=1))
        psum = ctx.enter_context(tc.psum_pool(name="psum", bufs=1))

        def sbuf(name, shape, dtype, tag=None):
            return keep.tile(shape, dtype, name=name, tag=tag or name, align_bytes=64)

        def multiply(acc, stationary, moving, start=True, stop=True):
            nc.tensor.matmul_mx(
                out=acc,
                lhsT=stationary[0].bitcast(FP8X4),
                lhsT_scale=stationary[1],
                rhs=moving[0].bitcast(FP8X4),
                rhs_scale=moving[1],
                start=start,
                stop=stop,
            )

        offs_t = lists.tile([P, S // LIST_ROWS], U16, name="offs_t")
        src_t = lists.tile([P, U // LIST_ROWS], U16, name="src_t")
        dst_t = lists.tile([P, U // LIST_ROWS], U16, name="dst_t")

        xs_all = sbuf("xs_all", [P, T], U8)
        xs = [sbuf(f"xs{g}", [P, S], U8) for g in range(PASSES)]
        nc.vector.memset(xs_all[QUADRANT : 2 * QUADRANT].bitcast(I32), 0)
        nc.vector.memset(xs_all[2 * QUADRANT :].bitcast(I32), 0)
        for g in range(PASSES):
            nc.gpsimd.memset(xs[g][:].bitcast(I32), 0)

        xw_all, xw, raw, late = {}, {}, {}, []

        def load_words(g):
            xw_all[g] = sbuf(f"xw_all{g}", [P, T], U32)
            nc.sync.dma_start(
                out=xw_all[g][:].bitcast(I32), in_=x_words[g].rearrange("p n t -> p (n t)").bitcast(I32)
            )

        def rows_of(a, g):
            return (w2, w1)[a][g * K_PASS : (g + 1) * K_PASS, :].rearrange("(p j) c -> p j c", j=PACK)

        def load_weight(a, g, tag=None):
            raw[a, g] = sbuf(f"raw{a}{g}", [P, PACK, H], F32, tag)
            nc.sync.dma_start(out=raw[a, g][:], in_=rows_of(a, g))

        def load_late(tag):
            m0, m1 = LATE_PIECES[len(late)]
            late.append(sbuf(f"late{m0}", [P, PACK, PACK * (m1 - m0)], F32, tag))
            nc.sync.dma_start(out=late[-1][:], in_=rows_of(E, 1)[:, :, PACK * m0 : PACK * m1])

        nc.sync.dma_start(offs_t[:], offs)
        nc.sync.dma_start(
            out=xs_all[:QUADRANT, :].bitcast(I32), in_=x_scales.rearrange("g r n -> (g r) n").bitcast(I32)
        )
        load_words(0)
        load_weight(E, 0)
        load_words(1)
        nc.sync.dma_start(src_t[:], src)
        nc.sync.dma_start(dst_t[:], dst)

        picked_scales = sbuf("picked_scales", [P, S], U8)
        weights, planes = {}, {}

        def gather_words(g):
            xw[g] = sbuf(f"xw{g}", [P, S], U32)
            nc.vector.tensor_copy(out=xw[g][:], in_=xw_all[g][:].indirect(offs_t[:]))

        def woven_tile(name, count):
            return sbuf(name, [P, count, P, PACK], BF16)

        def weave(source, first, woven, copy, m0=0, m1=P, base=0):
            dealt = source[:].rearrange("p j (m t) -> p m j t", t=PACK)[:, :, :, first : first + PAIR]
            copy(out=woven.rearrange("p t m j -> p m j t")[:, m0:m1], in_=dealt[:, m0 - base : m1 - base])

        def woven_pair(a, g, first, copy):
            woven = woven_tile(f"woven{a}{g}{first}", PAIR)
            weave(raw[a, g], first, woven[:], copy)
            return woven

        def quantise(name, woven, keys):
            words = sbuf(f"codes_{name}", [P, len(keys) * P], U32)
            planes[name] = sbuf(f"plane_{name}", [P, len(keys) * P], U8)
            nc.vector.quantize_mx(
                out=words[:].bitcast(FP8X4), scales=planes[name][:], in_=woven[:, :].rearrange("p t m j -> p (t m j)")
            )
            for n, key in enumerate(keys):
                weights[key] = words[:, n * P : (n + 1) * P], planes[name][:, n * P : (n + 1) * P]

        def pair_keys(a, g, first):
            return [(a, g, first + n) for n in range(PAIR)]

        def one_pass(acc, a, g, t, columns):
            multiply(acc[:], weights[a, g, t], (xw[g][:, columns], xs[g][:, columns]), g == 0, g == PASSES - 1)

        banks = {}

        def product_pass(a, g, t, h):
            if g == 0:
                banks[a, t, h] = psum.tile([P, BANK], F32, name=f"acc{a}{t}{h}", tag=f"bank{TILE_BANKS[a, t][h]}")
            one_pass(banks[a, t, h], a, g, t, slice(h * BANK, (h + 1) * BANK))

        def both_passes(a, t, h):
            for g in range(PASSES):
                product_pass(a, g, t, h)

        def lower_pair_pass(g):
            for t in range(PAIR):
                for h in range(HALVES):
                    product_pass(Y, g, t, h)

        quarters = [psum.tile([P, QUARTER], F32, name=f"quarter{b}", tag=f"bank{b}") for b in QUARTER_BANKS]

        def first_tile_pass(g):
            for n, acc in enumerate(quarters):
                one_pass(acc, E, g, 0, slice(n * QUARTER, (n + 1) * QUARTER))

        e_all = [sbuf(f"e_all{t}", [P, WIDE_WINDOW], F32) for t in range(PAIR)]
        for window in e_all:
            nc.gpsimd.memset(window[:, S:], 0.0)
        e_all.append(sbuf("e_all2", [P, S], F32))
        warm = keep.tile([P, 1], F32, name="warm")
        nc.scalar.activation(out=warm[:], in_=e_all[0][:, S : S + 1], func=SILU)
        y_all = [sbuf(f"y_all{t}", [P, S], F32) for t in range(PACK)]

        def empty_bank(a, t, h, copy):
            copy(out=(e_all, y_all)[a][t][:, h * BANK : (h + 1) * BANK], in_=banks[a, t, h][:])

        def empty_tile(a, t, copy):
            for h in range(HALVES):
                empty_bank(a, t, h, copy)

        fetched = {}

        def fetch(t, first, last, place):
            nc.scalar.activation(out=place, in_=e_all[t][:].indirect(entries(dst_t, first, last)), func=COPY)
            for at in range(first, last, HALF_EDGES):
                fetched[t, at] = place[:, at - first : at - first + HALF_EDGES]

        def place_scale_rows(g):
            for q in range(P // QUADRANT):
                to, at = QUADRANT * q, SCALE_ROWS * (P // QUADRANT * g + q)
                nc.sync.dma_start(
                    out=xs[g][to : to + SCALE_ROWS, :].bitcast(I32),
                    in_=picked_scales[at : at + SCALE_ROWS, :].bitcast(I32),
                )

        nc.vector.tensor_copy(out=picked_scales[:], in_=xs_all[:].indirect(offs_t[:]))
        place_scale_rows(0)
        gather_words(0)
        load_late("xs_all")
        load_late("xw_all0")
        place_scale_rows(1)
        e_lower = woven_pair(E, 0, 0, on_scalar)
        quantise("e0_upper", woven_pair(E, 0, PAIR, on_vector), pair_keys(E, 0, PAIR))
        quantise("e0_lower", e_lower, pair_keys(E, 0, 0))
        load_weight(Y, 0, f"raw{E}0")
        gather_words(1)
        load_weight(Y, 1, "xw_all1")
        first_tile_pass(0)
        for t, h in ((1, 0), (1, 1), (2, 0)):
            product_pass(E, 0, t, h)

        late_lower, late_upper = woven_tile("late_lower", PAIR), woven_tile("late_upper", PAIR)
        cut = LATE_PIECES[1][0]
        weave(late[0], 0, late_lower[:], on_scalar, 0, cut)
        weave(late[1], 0, late_lower[:], on_vector, cut, P, cut)
        quantise("e1_tile0", late_lower[:, :1], [(E, 1, 0)])
        first_tile_pass(1)
        quantise("e1_tile1", late_lower[:, 1:], [(E, 1, 1)])
        for h in range(HALVES):
            product_pass(E, 1, 1, h)
        weave(late[0], PAIR, late_upper[:], on_scalar, 0, SCALAR_SHARE)
        weave(late[1], PAIR, late_upper[:], on_vector, cut, P, cut)
        weave(late[0], PAIR, late_upper[:], on_vector, SCALAR_SHARE, cut)
        for n, acc in enumerate(quarters):
            copy = on_vector if n % 2 else on_scalar
            copy(out=e_all[0][:, n * QUARTER : (n + 1) * QUARTER], in_=acc[:])
        w3_codes = sbuf("w3_codes", [P, N], U32, "xs_all")
        nc.sync.dma_start(out=w3_codes[:].bitcast(I32), in_=w3_words[0].rearrange("p n t -> p (n t)").bitcast(I32))
        quantise("e1_upper", late_upper, pair_keys(E, 1, PAIR))
        fetch(0, 0, U, sbuf("fetched0", [P, U], F32)[:])
        product_pass(E, 1, 2, 0)
        for t, h in ((2, 1), (3, 0), (3, 1)):
            both_passes(E, t, h)

        empty_tile(E, 1, on_vector)
        y_lower = woven_pair(Y, 0, 0, on_vector)
        fetch(1, 0, U, sbuf("fetched1", [P, U], F32)[:])
        empty_bank(E, 2, 0, on_vector)
        empty_bank(E, 2, 1, on_scalar)
        fetch(2, 0, HALF_EDGES, sbuf("fetched2_early", [P, HALF_EDGES], F32)[:])
        quantise("y0_lower", y_lower, pair_keys(Y, 0, 0))
        lower_pair_pass(0)
        y_upper = woven_tile("y_upper", PASSES * PAIR)
        weave(raw[Y, 0], PAIR, y_upper[:, :PAIR], on_vector)
        y_lower = woven_pair(Y, 1, 0, on_vector)
        weave(raw[Y, 1], PAIR, y_upper[:, PAIR:], on_vector)
        quantise("y1_lower", y_lower, pair_keys(Y, 1, 0))
        lower_pair_pass(1)
        quantise("y_upper", y_upper, pair_keys(Y, 0, PAIR) + pair_keys(Y, 1, PAIR))
        empty_tile(Y, 0, on_vector)
        empty_bank(Y, 1, 0, on_vector)
        empty_bank(Y, 1, 1, on_scalar)
        e_all.append(sbuf("e_all3", [P, S], F32, "codes_y1_lower"))
        empty_tile(E, 3, on_scalar)
        for t in range(PAIR, PACK):
            for h in range(HALVES):
                both_passes(Y, t, h)
            empty_tile(Y, t, on_scalar)

        sums = sbuf("sums", [P, PACK * U - WIDE], F32)
        sums_by_half = [
            half.rearrange("p (t r) -> p t r", t=PACK)
            for half in (sums[:, PACK * HALF_EDGES - WIDE :], sums[:, : PACK * HALF_EDGES])
        ]

        def sums_of(t, first, last):
            h, at = divmod(first, HALF_EDGES)
            return sums_by_half[h][:, t, at : at + last - first]

        def join(t, first, last):
            at = first % HALF_EDGES
            nc.vector.tensor_tensor(
                out=sums_of(t, first, last),
                in0=y_all[t][:].indirect(entries(src_t, first, last)),
                in1=fetched[t, first - at][:, at : at + last - first],
                op=ADD,
            )

        for t in range(PAIR):
            join(t, 0, HALF_EDGES)
            join(t, HALF_EDGES, U)
        join(2, 0, HALF_EDGES)
        fetch(3, 0, HALF_EDGES, sums_of(2, HALF_EDGES, U))
        fetch(2, HALF_EDGES, U, sbuf("fetched2_late", [P, HALF_EDGES], F32, "plane_y_upper")[:])
        fetch(3, HALF_EDGES, U, sbuf("fetched3_late", [P, HALF_EDGES], F32, "codes_y_upper")[:])

        w3_plane = planes["y1_lower"]
        for q in range(P // QUADRANT):
            nc.sync.dma_start(
                out=w3_plane[QUADRANT * q : QUADRANT * q + SCALE_ROWS, :].bitcast(I32),
                in_=w3_scales[0, SCALE_ROWS * q : SCALE_ROWS * (q + 1), :].bitcast(I32),
            )

        out_v = out.rearrange("(b p) r -> p b r", p=P)
        spans = [(sum(PIECES[:n]), sum(PIECES[: n + 1])) for n in range(len(PIECES))]
        z, results = [], []

        def parts(n):
            step = PIECES[n] // 2 if spans[n][1] == U else PIECES[n]
            return [slice(at, at + step) for at in range(0, PIECES[n], step)]

        def activate(n):
            first = spans[n][0]
            z.append(sbuf(f"z{first}", [P, PIECES[n] * PACK], BF16))
            if first % WIDE == 0:
                join(PACK - 1, first, first + WIDE)
            for part in parts(n):
                nc.scalar.activation(
                    out=z[n][:, part.start * PACK : part.stop * PACK].rearrange("p (c i t) -> p c t i", i=PAIR, t=PACK),
                    in_=sums_of(slice(0, PACK), first + part.start, first + part.stop).rearrange(
                        "p t (c i) -> p c t i", i=PAIR
                    ),
                    func=SILU,
                )

        def product(n):
            first, width = spans[n][0], PIECES[n]
            z_codes, z_plane = sbuf(f"z_codes{first}", [P, width], U32), sbuf(f"z_plane{first}", [P, width], U8)
            in_a_bank = BLOCKS // len(RESULT_BANKS[n])
            accs = [
                psum.tile([P, in_a_bank, width], F32, name=f"result{first}_{b}", tag=f"bank{b}") for b in RESULT_BANKS[n]
            ]
            results.append(accs)
            for part in parts(n):
                nc.vector.quantize_mx(
                    out=z_codes[:, part].bitcast(FP8X4),
                    scales=z_plane[:, part],
                    in_=z[n][:, part.start * PACK : part.stop * PACK],
                )
                for b in range(BLOCKS):
                    cols = slice(b * P, (b + 1) * P)
                    multiply(
                        accs[b // in_a_bank][:, b % in_a_bank, part],
                        (w3_codes[:, cols], w3_plane[:, cols]),
                        (z_codes[:, part], z_plane[:, part]),
                    )

        def store(n, copies):
            first, last = spans[n]
            staged = sbuf(f"staged{first}", [P, BLOCKS, last - first], F32, f"z{last}" if last <= HALF_EDGES else None)
            in_a_bank, in_a_copy = BLOCKS // len(results[n]), BLOCKS // len(copies)
            for c, copy in enumerate(copies):
                rows = slice(c * in_a_copy, (c + 1) * in_a_copy)
                at = rows.start % in_a_bank
                copy(out=staged[:, rows], in_=results[n][rows.start // in_a_bank][:, at : at + in_a_copy])
                if PIECES[n] == WIDE:
                    nc.sync.dma_start(out=out_v[:, rows, first:last], in_=staged[:, rows])
            if PIECES[n] < WIDE:
                nc.sync.dma_start(out=out_v[:, :, first:last], in_=staged[:])

        activate(0)
        activate(1)
        join(2, HALF_EDGES, U)
        activate(2)
        product(0)
        activate(3)
        activate(4)
        for n in range(1, len(PIECES)):
            product(n)
        store(0, (on_vector, on_vector))
        store(1, (on_vector, on_scalar))
        store(2, (on_scalar, on_scalar))
        store(3, (on_vector,))
        store(4, (on_vector, on_scalar))
